import numpy as np
import ml_dtypes


def mxq(x, axis, fmt="e4m3"):
    dtype, down = {"e4m3": (ml_dtypes.float8_e4m3fn, 7), "e5m2": (ml_dtypes.float8_e5m2, 14)}[fmt]
    v = np.moveaxis(np.asarray(x, np.float32).astype(ml_dtypes.bfloat16).astype(np.float64), axis, -1)
    blocks = v.reshape(v.shape[:-1] + (-1, 32))
    amax = np.abs(blocks).max(-1, keepdims=True)
    byte = np.maximum(np.where(amax > 0, np.frexp(amax)[1] - 1 + 127, 0) - down, 1)
    scale = np.exp2(byte - 127.0)
    codes = (blocks / scale).astype(np.float32).astype(dtype).astype(np.float64)
    return np.moveaxis((codes * scale).reshape(v.shape), -1, axis)


WIDE = False


def mx_kscale(k):
    if not WIDE:
        return np.ones(k)
    levels = np.array([10, -10, 5, -5, 0])
    if k % 512:
        return np.exp2(np.random.permutation(np.resize(levels, k // 32))).repeat(32)
    a = np.empty((k // 512, 16))
    for p in range(k // 512):
        a[p, :8] = np.random.permutation(np.resize(levels, 8))
        for g in range(8):
            far = levels[np.abs(levels - a[p, g]) >= 10]
            a[p, g + 8] = far[np.random.randint(len(far))]
    return np.exp2(a.ravel()).repeat(32)


BF16 = ml_dtypes.bfloat16


def bf(x):
    return np.asarray(x, np.float32).astype(BF16)


def f64(x):
    return np.asarray(x).astype(np.float64)

def planes(Y):
    n, m = Y.shape
    b = f64(bf(Y)).reshape(n // 32, 32, m)
    amax = np.abs(b).max(1)
    byte = np.clip(np.where(amax > 0, np.frexp(amax)[1] - 1 + 127 - 7, 1), 1, 254)
    codes = (b * np.exp2(127.0 - byte)[:, None, :]).reshape(n, m).astype(np.float32).astype(ml_dtypes.float8_e4m3fn).view(np.uint8)
    words = codes.reshape(n // 512, 128, 4, m).transpose(0, 1, 3, 2)
    return np.ascontiguousarray(words), np.ascontiguousarray(byte.astype(np.uint8).reshape(n // 512, 16, m))


T, D, F, O, E = 512, 1024, 1024, 1024, 4


def erf(a):
    c = np.clip(a, -6.0, 6.0)
    z = 2.0 * c * c
    term = c
    total = c
    for n in range(1, 150):
        term = term * z / (2.0 * n + 1.0)
        total = total + term
    return np.where(np.abs(a) <= 6.0, 2.0 / np.sqrt(np.pi) * np.exp(-c * c) * total, np.sign(a))


def gelu_erf(u):
    return 0.5 * u * (1.0 + erf(u / np.sqrt(2.0)))


def setup_inputs():
    s, t = mx_kscale(D), mx_kscale(F)
    return {
        "x": bf(np.random.standard_normal((T, D))),
        "wg": bf(np.random.standard_normal((D, E)) * 1.5 / np.sqrt(D)),
        "r1": bf(np.random.standard_normal((E, D)) * s),
        "w1": bf(np.random.standard_normal((D, F)) / np.sqrt(D) / s[:, None]),
        "s1": bf(np.random.standard_normal((E, F))),
        "r2": bf(np.random.standard_normal((E, F)) * t),
        "w2": bf(np.random.standard_normal((F, O)) * 2.0 / np.sqrt(F) / t[:, None]),
    }


def core(x, wg, r1, w1, s1, r2, w2):
    x, wg, r1, w1, s1, r2, w2 = f64(x), f64(wg), f64(r1), f64(w1), f64(s1), f64(r2), f64(w2)
    logits = np.sum(x[:, None, :] * wg.T[None, :, :], axis=-1)
    e = np.exp(logits - logits.max(-1, keepdims=True))
    g = e / e.sum(-1, keepdims=True)
    xe = x[None, :, :] * r1[:, None, :]
    p = mxq(xe.reshape(E * T, D), 1, "e4m3") @ mxq(w1, 0, "e4m3")
    u = p.reshape(E, T, F) * s1[:, None, :]
    h = gelu_erf(u)
    gate = g.T[:, :, None]
    m = np.sum(gate * h * r2[:, None, :], axis=0)
    return mxq(m, 1, "e4m3") @ mxq(w2, 0, "e4m3")


def reference(x, wg, r1, w1, s1, r2, w2):
    R_out = core(x, wg, r1, w1, s1, r2, w2)
    words, scales = planes(R_out.T)
    return R_out, words, scales

@@ -1,0 +1,499 @@
+from contextlib import ExitStack
+
+import concourse.mybir as mybir
+from concourse.masks import make_identity
+
+T, D, F, O, E = 512, 1024, 1024, 1024, 4
+FLOPS = 2 * E * T * D * F + 2 * T * F * O + 2 * T * D * E
+
+F32 = mybir.dt.float32
+BF16 = mybir.dt.bfloat16
+I32 = mybir.dt.int32
+U32 = mybir.dt.uint32
+U8 = mybir.dt.uint8
+FP8X4 = mybir.dt.float8_e4m3fn_x4
+ALU = mybir.AluOpType
+ACT = mybir.ActivationFunctionType
+AX = mybir.AxisListType
+
+P = 128
+BLOCKS = [(0, 128), (128, 128), (256, 128), (384, 128)]
+STEPS = [(tok0, n, fg) for tok0, n in BLOCKS for fg in range(2)]
+H_BUFS = 9
+W_BUFS = 5
+QP_LAG = 3
+LEAD = 5
+SECOND_PER_UNIT = 1
+PIECES = [0, 0, 0, 1, 2, 3, 4, 5, 6, 6, 7, 7, 8]
+
+
+def tile_batchensemblerankoneexpertmixturemlp_x1_kernel(tc, x, wg, r1, w1, s1, r2, w2, out_0, out_1, out_2):
+    nc = tc.nc
+    with ExitStack() as ctx:
+        keep = ctx.enter_context(tc.tile_pool(name="keep", bufs=1))
+        psum = ctx.enter_context(tc.psum_pool(name="psum", bufs=1))
+        ctx.enter_context(tc.manual_schedule())
+
+        def tiles(name, count, shape, dtype):
+            return [keep.tile(shape, dtype, name="%s%d" % (name, i), align_bytes=64) for i in range(count)]
+
+        bank = [psum.tile([P, 512], F32, name="bank%d" % i) for i in range(8)]
+        ident, = tiles("ident", 1, [P, P], F32)
+        warm_in, warm_out = tiles("warm", 2, [P, 1], F32)
+        par_rows = tiles("par_rows", 2, [P, 512], BF16)
+        r1_col, = tiles("r1_col", 1, [P, 8, 2, 2], BF16)
+        sr_col, = tiles("sr_col", 1, [P, 16, 4], F32)
+        wg_sb, = tiles("wg_sb", 1, [P, 2, 4, E], BF16)
+        x_rows = tiles("x_rows", 4, [P, 2, 512], BF16)
+        x_t, = tiles("x_t", 1, [P, 2, T, 4], BF16)
+        xe = tiles("xe", 7, [P, T, 4], BF16)
+        xe_codes = tiles("xe_codes", E, [P, 2, T], U32)
+        xe_scales = tiles("xe_scales", E, [P, 2, T], U8)
+        w_raw = {}
+        for which in range(2):
+            for g in range(2):
+                for c in range(2):
+                    w_raw[which, g, c], = tiles("w_raw%d%d%d_" % (which, g, c), 1, [P, 4, 512], BF16)
+        w_grouped = tiles("w_grouped", W_BUFS, [P, 512, 4], BF16)
+        w_codes = tiles("w_codes", 2, [P, 2, 1024], U32)
+        w_scales = tiles("w_scales", 2, [P, 2, 1024], U8)
+        gate_max, gate_sum, gate_inv = tiles("gate_a", 3, [P, 4], F32)
+        gate_d, gate_th, gate_den, gate_rden, gate_ex, gate = tiles("gate_b", 6, [P, 4, E], F32)
+        h = tiles("h", H_BUFS, [P, 512], F32)
+        term1 = tiles("term1_", 3, [P, 512], F32)
+        acc, = tiles("acc", 1, [P, 8, T], F32)
+        term2 = tiles("term2_", 2, [P, 4, 256], F32)
+        term3 = tiles("term3_", 2, [P, 4, 256], F32)
+        part, = tiles("part", 1, [P, 4, 256], F32)
+        m_bf = tiles("m_bf", 2, [P, 256, 4], BF16)
+        m_codes, = tiles("m_codes", 1, [P, 2, T], U32)
+        m_scales, = tiles("m_scales", 1, [P, 2, T], U8)
+        out_sb = tiles("out_sb", 3, [P, O], F32)
+        p_bf = tiles("p_bf", 4, [P, P, 4], BF16)
+        p_codes, = tiles("p_codes", 1, [P, 2, T], U32)
+        p_scales, = tiles("p_scales", 1, [P, 2, T], U8)
+
+        ops = {}
+
+        def op(name, needs, fn):
+            ops[name] = (list(needs), fn)
+
+        def quantize(codes, scales, grouped):
+            nc.vector.quantize_mx(out=codes.bitcast(FP8X4), scales=scales, in_=grouped.rearrange("p c t -> p (c t)"))
+
+        def mx_group(out, lhs_codes, lhs_scales, lhs_cols, rhs_codes, rhs_scales, rhs_cols, passes=(0, 1)):
+            for g in passes:
+                nc.tensor.matmul_mx(
+                    out=out,
+                    lhsT=lhs_codes[:, g, lhs_cols].bitcast(FP8X4), lhsT_scale=lhs_scales[:, g, lhs_cols],
+                    rhs=rhs_codes[:, g, rhs_cols].bitcast(FP8X4), rhs_scale=rhs_scales[:, g, rhs_cols],
+                    start=(g == 0), stop=(g == 1))
+
+        w1_chunks = [(0, 0, 0), (0, 1, 0), (0, 0, 1), (0, 1, 1)]
+        w2_chunks = [(1, 0, 0), (1, 1, 0), (1, 0, 1), (1, 1, 1)]
+
+        def step_banks(k):
+            return STEPS[k][1] // P
+
+        def a_units():
+            return [("A", ft, e) for ft in range(8) for e in range(2)]
+
+        def b_units(k, e):
+            return [("B", k, e, i) for i in range(step_banks(k))]
+
+        b_order = b_units(0, 2)
+        for k in range(len(STEPS)):
+            b_order = b_order + b_units(k, 3) + (b_units(k + 1, 2) if k + 1 < len(STEPS) else [])
+        units = a_units() + b_order
+
+        def gelus(us):
+            return [("gelu", u) for u in us]
+
+        def stts(us):
+            return [("stt", u) for u in us]
+
+        def mms(us):
+            return [("mm", u) for u in us]
+
+        au = a_units()
+        n_steps = len(STEPS)
+        tiles_after = {k: list(range(tok0 // P, (tok0 + n) // P)) for k, (tok0, n, fg) in enumerate(STEPS) if fg == 1}
+        last_j = T // P - 1
+
+        sync_q = [("x_load", 0), ("par_load", 0)] + [("x_load", b) for b in range(1, 4)] + [("w_load", c) for c in w1_chunks + w2_chunks]
+        for tok0, n in BLOCKS[:-1]:
+            sync_q += [("st_o", j, None) for j in range(tok0 // P, (tok0 + n) // P)] + [("st_p", tok0, n)]
+        sync_q += [("st_o", last_j, 0), ("st_o", last_j, 1), ("st_p",) + BLOCKS[-1], ("st_s", 0), ("st_s", 1)]
+
+        pool_q = [("ident",), ("wg_load",), ("par_load", 1), ("par_load", 2), ("il", w1_chunks[0], 0, 4), ("il", w1_chunks[2], 0, 4)]
+        pool_q += [("add1", ft) for ft in range(8)] + [("add2", k) for k in range(n_steps)]
+
+        vec_q = [("memset",), ("par_copy", 0)]
+        vec_q += [("mult", e, b) for b in range(2) for e in range(4)]
+        vec_q += [("mult", e, 2) for e in range(3)] + [("par_copy", 1)]
+        vec_q += [("mult", 0, 3), ("mult", 1, 3), ("mult", 2, 3)]
+        vec_q += [("q_xe", 0, 0), ("gate", 0), ("q_xe", 0, 1), ("gate", 1), ("q_w", w1_chunks[0]), ("q_w", w1_chunks[1]), ("gate", 3),
+                  ("q_xe", 1, 0), ("gate", 4), ("q_xe", 1, 1), ("gate", 5), ("q_w", w1_chunks[2]), ("gate", 6),
+                  ("q_w", w1_chunks[3]), ("gate", 7), ("q_xe", 2, 0), ("gate", 8), ("q_xe", 2, 1), ("q_xe", 3, 0), ("q_w", w2_chunks[0])]
+        a_before = {1: [("mult", 3, 2)], 2: [("mult", 3, 3)]}
+        a_after = {3: [("q_xe", 3, 1)], 4: [("q_w", w2_chunks[1])], 6: [("q_w", w2_chunks[2])]}
+        for ft in range(8):
+            vec_q += a_before.get(ft, []) + stts(au[2 * ft: 2 * ft + 2]) + a_after.get(ft, [])
+        vec_q += stts(b_units(0, 2))
+        b_port = {0: [("q_w", w2_chunks[3])]}
+        vec_copies = [("cp_p", last_j - 1, 0), ("cp_p", last_j, 1), ("cp_o", last_j, 1)]
+        for k in range(n_steps):
+            vec_q += stts(b_units(k, 3)) + (stts(b_units(k + 1, 2)) if k + 1 < n_steps else [])
+            if k == n_steps - 1:
+                vec_q += [("cp_p", last_j - 1, 0)]
+            vec_q += ([("q_m", k - 1)] if k else []) + b_port.get(k, [])
+            if k < n_steps - 1:
+                vec_q += [("q_p", j, og) for j in tiles_after.get(k - QP_LAG, []) for og in range(2)]
+            vec_q += [("final", k)]
+        late = [("q_p", j, og) for j in range(last_j) for og in range(2) if ("q_p", j, og) not in vec_q]
+        vec_q += late[:1] + [("q_m", n_steps - 1)] + late[1:]
+        vec_q += [("cp_o", last_j, 1), ("cp_p", last_j, 1), ("q_p", last_j, 0), ("q_p", last_j, 1)]
+
+        def vec_position(k):
+            return sum(1 for name in vec_q[: vec_q.index(("q_m", k))] if name[0] == "stt" and name[1][0] == "B")
+
+        second_at = {}
+        for k, js in tiles_after.items():
+            at = min(vec_position(k) + LEAD, len(b_order))
+            todo = [(kind, j, og) for kind in ("op" if k == n_steps - 1 else "po") for j in js for og in range(2)]
+            for i, item in enumerate(todo):
+                second_at.setdefault(min(at + i // SECOND_PER_UNIT, len(b_order)), []).append(item)
+
+        act_q = [("warm",)]
+        act_q += [("x_copy", 1), ("x_copy", 0), ("x_copy", 2), ("x_copy", 3)]
+        act_q += [("il", w1_chunks[1], 0, 4), ("il", w1_chunks[3], 0, 4), ("il", w2_chunks[0], 0, 2), ("gate", 2)]
+        pieces = [("il", c, q, q + 1) for c in w2_chunks[2:] for q in range(4)]
+        act_q += [("il", w2_chunks[0], 2, 4), ("il", w2_chunks[1], 0, 4)]
+        for ft in range(8):
+            act_q += pieces[PIECES[ft]: PIECES[ft + 1]] + gelus(au[2 * ft: 2 * ft + 2])
+        pe_q = [("par_turn", 0), ("x_turn", 0), ("x_turn", 1), ("x_turn", 2), ("x_turn", 3), ("par_turn", 1), ("logits",)]
+        pe_q += mms(au[0:4]) + [("spread", 0), ("spread", 1)] + mms(au[4:12]) + [("spread", 2), ("spread", 3)] + mms(au[12:])
+        for i in range(len(b_order) + 1):
+            pe_q += [("mm_" + kind, j, og) for kind, j, og in second_at.get(i, [])] + mms(b_order[i: i + 1])
+            act_q += [("cp_" + kind, j, og) for kind, j, og in second_at.get(i - 1, []) if ("cp_" + kind, j, og) not in vec_copies]
+            act_q += pieces[PIECES[8 + min(i, len(PIECES) - 9)]: PIECES[8 + min(i + 1, len(PIECES) - 9)]] + gelus(b_order[i: i + 1])
+        at = pe_q.index(("mm_o", last_j, 0))
+        pe_q = pe_q[:at] + [("mm_early", last_j, 0), ("mm_early", last_j, 1)] + pe_q[at:]
+        act_q += [("cp_" + kind, j, og) for kind, j, og in second_at[len(b_order)] if ("cp_" + kind, j, og) not in vec_copies]
+        act_q += [("st_s", 2), ("st_s", 3)]
+
+        bank_of = {("par_turn", 0): 6, ("par_turn", 1): 6, ("logits",): 7, ("spread", 0): 4, ("spread", 1): 5, ("spread", 2): 2, ("spread", 3): 3}
+        for b in range(4):
+            bank_of["x_turn", b] = b
+        ring_a, ring_b, ring_out = [6, 7, 0, 1], [6, 7, 0], [1, 4, 5]
+        for i, u in enumerate(au):
+            bank_of["mm", u] = ring_a[i % 4]
+        for i, u in enumerate(b_order):
+            bank_of["mm", u] = ring_b[i % 3]
+        second = [name for name in pe_q if name[0] in ("mm_p", "mm_o")]
+        for i, name in enumerate(second[:-4]):
+            bank_of[name] = ring_out[i % 3]
+        for name, b in zip(second[-4:], [6, 7, 0, 2]):
+            bank_of[name] = b
+        for og in range(2):
+            bank_of["mm_early", last_j, og] = bank_of["mm_o", last_j, og]
+
+        def readers(name):
+            kind = name[0]
+            if kind == "x_turn":
+                return [("x_copy", name[1])] + [("mult", e, name[1]) for e in range(E)]
+            if kind == "par_turn":
+                return [("par_copy", name[1])]
+            if kind == "logits":
+                return [("gate", 0), ("gate", 1)]
+            if kind == "spread":
+                return [("stt", u) for u in units if u[2] == name[1]]
+            if kind == "mm_early":
+                return []
+            if kind == "mm":
+                return [("gelu", name[1])]
+            return [("cp_p" if kind == "mm_p" else "cp_o",) + name[1:]]
+
+        bank_free = {}
+        holder = {}
+        for name in pe_q:
+            b = bank_of[name]
+            bank_free[name] = readers(holder[b]) if b in holder else []
+            holder[b] = name
+
+        def memsets():
+            nc.vector.memset(par_rows[0][:].bitcast(I32), 0)
+            nc.vector.memset(par_rows[1][:].bitcast(I32), 0)
+            nc.vector.memset(warm_in[:], 0.0)
+
+        op(("memset",), [], memsets)
+        op(("ident",), [], lambda: make_identity(nc, ident[:]))
+        op(("warm",), [("memset",)], lambda: nc.scalar.activation(out=warm_out[:], in_=warm_in[:], func=ACT.Gelu))
+        for i, vec in enumerate((r1, s1, r2)):
+            op(("par_load", i), [("memset",)], lambda i=i, vec=vec: (nc.gpsimd if i else nc.sync).dma_start(
+                out=par_rows[min(i, 1)][8 * (i // 2): 8 * (i // 2) + 8, :], in_=vec.rearrange("e (g k) -> (e g) k", g=2)))
+        op(("wg_load",), [], lambda: nc.gpsimd.dma_start(
+            out=wg_sb[:].rearrange("p g t e -> p g (t e)"), in_=wg.rearrange("(g p t) e -> p g (t e)", g=2, t=4)))
+        for b in range(4):
+            g, half = divmod(b, 2)
+            op(("x_load", b), [], lambda b=b, g=g, half=half: nc.sync.dma_start(
+                out=x_rows[b][:],
+                in_=x[256 * half: 256 * half + 256, 512 * g: 512 * g + 512].rearrange("(j p) d -> p j d", p=P)))
+        for chunk in w1_chunks + w2_chunks:
+            which, g, c = chunk
+            op(("w_load", chunk), [], lambda chunk=chunk, which=which, g=g, c=c: nc.sync.dma_start(
+                out=w_raw[chunk][:],
+                in_=(w1, w2)[which][512 * g: 512 * g + 512, 512 * c: 512 * c + 512].rearrange("(p j) f -> p j f", j=4)))
+
+        def x_turn(b):
+            words = x_rows[b][:].bitcast(F32)
+            for j in range(2):
+                for u in range(2):
+                    nc.tensor.transpose(bank[b][:, 256 * u + P * j: 256 * u + P * j + P], words[:, j, u:256:2], ident[:])
+
+        def par_turn(i):
+            words = par_rows[i][:].bitcast(F32)
+            for u in range(2):
+                nc.tensor.transpose(bank[6][:, P * u: P * u + P], words[:, u:256:2], ident[:])
+
+        def par_copy(i):
+            cols = bank[6][:, 0:256].bitcast(BF16).rearrange("p (u r c) -> p r u c", u=2, c=2)
+            if i == 0:
+                nc.vector.tensor_copy(out=r1_col[:], in_=cols[:, 0:8])
+            else:
+                nc.vector.tensor_copy(out=sr_col[:].rearrange("p r (u c) -> p r u c", u=2), in_=cols[:, 0:16])
+
+        def x_copy(b):
+            g, half = divmod(b, 2)
+            dst = x_t[:, g, 256 * half: 256 * half + 256, :].rearrange("p k t -> p (k t)").bitcast(F32)
+            nc.scalar.copy(out=dst.rearrange("p (k u) -> p k u", u=2), in_=bank[b][:].rearrange("p (u k) -> p k u", u=2))
+
+        def xe_tile(e, g):
+            return xe[(4 * g + e) % 7]
+
+        def mult(e, b):
+            g, half = divmod(b, 2)
+            nc.vector.tensor_tensor(
+                out=xe_tile(e, g)[:, 256 * half: 256 * half + 256, :].rearrange("p k (u c) -> p k u c", u=2),
+                in0=bank[b][:].bitcast(BF16).rearrange("p (u k c) -> p k u c", u=2, c=2),
+                in1=r1_col[:, 2 * e + g].unsqueeze(1).to_broadcast([P, 256, 2, 2]),
+                op=ALU.mult)
+
+        for b in range(4):
+            op(("x_turn", b), [("x_load", b), ("ident",)], lambda b=b: x_turn(b))
+            op(("x_copy", b), [("x_turn", b)] + ([("mult", e, 0) for e in range(E)] if b == 0 else []), lambda b=b: x_copy(b))
+            for e in range(E):
+                needs = [("x_turn", b), ("par_copy", 0)] + ([("x_copy", b)] if b else [])
+                if e == 3 and b >= 2:
+                    needs.append(("q_xe", 0, 0))
+                op(("mult", e, b), needs, lambda e=e, b=b: mult(e, b))
+        for i in range(2):
+            op(("par_turn", i), [("par_load", i), ("par_load", 2 * i), ("ident",)], lambda i=i: par_turn(i))
+            op(("par_copy", i), [("par_turn", i)], lambda i=i: par_copy(i))
+        for e in range(E):
+            for g in range(2):
+                op(("q_xe", e, g), [("mult", e, 2 * g), ("mult", e, 2 * g + 1)], lambda e=e, g=g: quantize(
+                    xe_codes[e][:, g, :], xe_scales[e][:, g, :], xe_tile(e, g)[:]))
+
+        il_names = [name for name in pool_q + act_q if name[0] == "il"]
+        chunk_order = [name[1] for name in vec_q if name[0] == "q_w"]
+
+        def interleave(chunk, q0, q1):
+            dst = w_grouped[chunk_order.index(chunk) % W_BUFS]
+            if ("il", chunk, q0, q1) in pool_q:
+                nc.gpsimd.tensor_scalar(
+                    out=dst[:].rearrange("p (t m) j -> p t m j", t=4),
+                    in0=w_raw[chunk][:].rearrange("p j (m t) -> p t m j", t=4),
+                    scalar1=1.0, scalar2=0.0, op0=ALU.mult, op1=ALU.add)
+            else:
+                nc.scalar.copy(
+                    out=dst[:].rearrange("p (t a i) j -> p a t i j", t=4, i=2)[:, 16 * q0: 16 * q1],
+                    in_=w_raw[chunk][:].rearrange("p j (a i t) -> p a t i j", t=4, i=2)[:, 16 * q0: 16 * q1])
+
+        for name in il_names:
+            n = chunk_order.index(name[1])
+            op(name, [("w_load", name[1])] + ([("q_w", chunk_order[n - W_BUFS])] if n >= W_BUFS else []),
+               lambda name=name: interleave(*name[1:]))
+        for n, chunk in enumerate(chunk_order):
+            which, g, c = chunk
+            op(("q_w", chunk), [name for name in il_names if name[1] == chunk], lambda n=n, which=which, g=g, c=c: quantize(
+                w_codes[which][:, g, 512 * c: 512 * c + 512], w_scales[which][:, g, 512 * c: 512 * c + 512], w_grouped[n % W_BUFS][:]))
+
+        logits_ps = bank[7][:, 0:16].rearrange("p (j e) -> p j e", e=E)
+
+        def logits():
+            for j in range(4):
+                for g in range(2):
+                    for t in range(4):
+                        nc.tensor.matmul(logits_ps[:, j, :], lhsT=x_t[:, g, P * j: P * j + P, t], rhs=wg_sb[:, g, t, :],
+                                         start=(g == 0 and t == 0), stop=(g == 1 and t == 3))
+
+        def over_experts(col):
+            return col[:].unsqueeze(2).to_broadcast([P, 4, E])
+
+        def flat(tile):
+            return tile[:].rearrange("p j e -> p (j e)")
+
+        op(("logits",), [("x_copy", b) for b in range(4)] + [("wg_load",)], logits)
+        gate_steps = [
+            lambda: nc.vector.tensor_reduce(out=gate_max[:], in_=logits_ps, axis=AX.X, op=ALU.max),
+            lambda: nc.vector.tensor_tensor(out=gate_d[:], in0=logits_ps, in1=over_experts(gate_max), op=ALU.subtract),
+            lambda: nc.scalar.activation(out=flat(gate_th), in_=flat(gate_d), func=ACT.Tanh, scale=0.5),
+            lambda: nc.vector.tensor_scalar(out=flat(gate_den), in0=flat(gate_th), scalar1=-1.0, scalar2=1.0,
+                                            op0=ALU.mult, op1=ALU.add),
+            lambda: nc.vector.reciprocal(out=flat(gate_rden), in_=flat(gate_den)),
+            lambda: nc.vector.scalar_tensor_tensor(out=flat(gate_ex), in0=flat(gate_th), scalar=1.0, in1=flat(gate_rden),
+                                                   op0=ALU.add, op1=ALU.mult),
+            lambda: nc.vector.tensor_reduce(out=gate_sum[:], in_=gate_ex[:], axis=AX.X, op=ALU.add),
+            lambda: nc.vector.reciprocal(out=gate_inv[:], in_=gate_sum[:]),
+            lambda: nc.vector.tensor_tensor(out=gate[:], in0=gate_ex[:], in1=over_experts(gate_inv), op=ALU.mult),
+        ]
+        for i, fn in enumerate(gate_steps):
+            op(("gate", i), [("gate", i - 1) if i else ("logits",)], fn)
+
+        def spread(e):
+            for j in range(4):
+                nc.tensor.transpose(bank[bank_of["spread", e]][:, P * j: P * j + P],
+                                    gate[:, j, e: e + 1].to_broadcast([P, P]), ident[:])
+
+        for e in range(E):
+            op(("spread", e), [("gate", 8)], lambda e=e: spread(e))
+
+        def unit_parts(u):
+            if u[0] == "A":
+                return [(u[1], 0, T, 0)]
+            tok0, n, fg = STEPS[u[1]]
+            per_bank = 512 // n
+            return [(4 * fg + per_bank * u[3] + i, tok0, n, n * i) for i in range(per_bank)]
+
+        def column(row0, e, ft):
+            return sr_col[:, row0 + 2 * e + ft // 4, ft % 4: ft % 4 + 1]
+
+        def mm(u):
+            e = u[2]
+            for ft, tok0, n, col in unit_parts(u):
+                mx_group(bank[bank_of["mm", u]][:, col: col + n], w_codes[0], w_scales[0], slice(P * ft, P * ft + P),
+                         xe_codes[e], xe_scales[e], slice(tok0, tok0 + n))
+
+        def gelu(u):
+            for ft, tok0, n, col in unit_parts(u):
+                nc.scalar.activation(out=h[units.index(u) % H_BUFS][:, col: col + n], in_=bank[bank_of["mm", u]][:, col: col + n],
+                                     func=ACT.Gelu, scale=column(0, u[2], ft))
+
+        def stt(u):
+            e = u[2]
+            for ft, tok0, n, col in unit_parts(u):
+                if e == 0:
+                    dst = acc[:, ft, :]
+                elif e == 1:
+                    dst = term1[ft % 3][:]
+                else:
+                    dst = (term2, term3)[e - 2][u[1] % 2][:, ft % 4, 0:n]
+                nc.vector.scalar_tensor_tensor(
+                    out=dst, in0=h[units.index(u) % H_BUFS][:, col: col + n], scalar=column(8, e, ft),
+                    in1=bank[bank_of["spread", e]][:, tok0: tok0 + n], op0=ALU.mult, op1=ALU.mult)
+
+        for i, u in enumerate(units):
+            e = u[2]
+            fg = u[1] // 4 if u[0] == "A" else STEPS[u[1]][2]
+            op(("mm", u), [("q_xe", e, 0), ("q_xe", e, 1), ("q_w", (0, 0, fg)), ("q_w", (0, 1, fg))], lambda u=u: mm(u))
+            op(("gelu", u), [("mm", u), ("par_copy", 1)] + ([("stt", units[i - H_BUFS])] if i >= H_BUFS else []), lambda u=u: gelu(u))
+            needs = [("gelu", u), ("spread", e)]
+            if e == 1 and u[1] >= 3:
+                needs.append(("add1", u[1] - 3))
+            if e >= 2 and u[1] >= 2:
+                needs.append(("add2" if e == 2 else "final", u[1] - 2))
+            op(("stt", u), needs, lambda u=u: stt(u))
+
+        def add2(k):
+            tok0, n, fg = STEPS[k]
+            nc.gpsimd.tensor_tensor(out=part[:, :, 0:n], in0=acc[:, 4 * fg: 4 * fg + 4, tok0: tok0 + n],
+                                    in1=term2[k % 2][:, :, 0:n], op=ALU.add)
+
+        def final(k):
+            n = STEPS[k][1]
+            nc.vector.tensor_tensor(
+                out=m_bf[k % 2][:, 0:n, :].rearrange("p (c i) t -> p c t i", i=4),
+                in0=part[:, :, 0:n].rearrange("p t (c i) -> p c t i", i=4),
+                in1=term3[k % 2][:, :, 0:n].rearrange("p t (c i) -> p c t i", i=4), op=ALU.add)
+
+        for ft in range(8):
+            op(("add1", ft), stts(au[2 * ft: 2 * ft + 2]), lambda ft=ft: nc.gpsimd.tensor_tensor(
+                out=acc[:, ft, :], in0=acc[:, ft, :], in1=term1[ft % 3][:], op=ALU.add))
+        for k, (tok0, n, fg) in enumerate(STEPS):
+            op(("add2", k), stts(b_units(k, 2)) + [("add1", 7)] + ([("final", k - 1)] if k else []), lambda k=k: add2(k))
+            op(("final", k), stts(b_units(k, 3)) + [("add2", k)] + ([("q_m", k - 2)] if k >= 2 else []), lambda k=k: final(k))
+            op(("q_m", k), [("final", k)], lambda k=k, tok0=tok0, n=n, fg=fg: quantize(
+                m_codes[:, fg, tok0: tok0 + n], m_scales[:, fg, tok0: tok0 + n], m_bf[k % 2][:, 0:n, :]))
+
+        def mm_p(j, og):
+            for t in range(4):
+                c0 = 512 * og + P * t
+                mx_group(bank[bank_of["mm_p", j, og]][:, P * t: P * t + P], w_codes[1], w_scales[1], slice(c0, c0 + P),
+                         m_codes, m_scales, slice(P * j, P * j + P))
+
+        def mm_o(j, og, passes):
+            mx_group(bank[bank_of["mm_o", j, og]][:], m_codes, m_scales, slice(P * j, P * j + P),
+                     w_codes[1], w_scales[1], slice(512 * og, 512 * og + 512), passes)
+
+        def copy_on(name, out, in_):
+            if name in vec_q:
+                nc.vector.tensor_copy(out=out, in_=in_)
+            else:
+                nc.scalar.copy(out=out, in_=in_)
+
+        def cp_p(j, og):
+            copy_on(("cp_p", j, og), p_bf[(2 * j + og) % 4][:],
+                    bank[bank_of["mm_p", j, og]][:].rearrange("p (t k) -> p k t", t=4))
+
+        def cp_o(j, og):
+            copy_on(("cp_o", j, og), out_sb[j % 3][:, 512 * og: 512 * og + 512].rearrange("p (m t) -> p m t", t=4),
+                    bank[bank_of["mm_o", j, og]][:].rearrange("p (t m) -> p m t", t=4))
+
+        def st_o(j, og):
+            cols = slice(0, O) if og is None else slice(512 * og, 512 * og + 512)
+            nc.sync.dma_start(out=out_0[P * j: P * j + P, cols], in_=out_sb[j % 3][:, cols])
+
+        words_out = out_1.rearrange("g p m t -> p g (m t)").bitcast(I32)
+        scales_out = out_2.rearrange("g q m -> q g m").bitcast(I32)
+
+        def st_s(q):
+            engine = nc.sync if ("st_s", q) in sync_q else nc.scalar
+            engine.dma_start(out=scales_out[4 * q: 4 * q + 4], in_=p_scales[32 * q: 32 * q + 4].bitcast(I32))
+
+        for j in range(4):
+            last = max(k for k, (tok0, n, fg) in enumerate(STEPS) if tok0 <= P * j)
+            ready = [("q_m", last - 1), ("q_m", last)] + [("q_w", c) for c in w2_chunks]
+            for og in range(2):
+                op(("mm_p", j, og), ready, lambda j=j, og=og: mm_p(j, og))
+                op(("mm_o", j, og), ready, lambda j=j, og=og: mm_o(j, og, (1,) if j == last_j else (0, 1)))
+                op(("mm_early", j, og), ready[:1] + ready[2:], lambda j=j, og=og: mm_o(j, og, (0,)))
+                op(("cp_p", j, og), [("mm_p", j, og)] + ([("q_p", j - 2, og)] if j >= 2 else []), lambda j=j, og=og: cp_p(j, og))
+                op(("cp_o", j, og), [("mm_o", j, og)] + ([("st_o", 0, None)] if j == 3 else []), lambda j=j, og=og: cp_o(j, og))
+                op(("q_p", j, og), [("cp_p", j, og)], lambda j=j, og=og: quantize(
+                    p_codes[:, og, P * j: P * j + P], p_scales[:, og, P * j: P * j + P], p_bf[(2 * j + og) % 4][:]))
+                op(("st_o", j, og), [("cp_o", j, og)], lambda j=j, og=og: st_o(j, og))
+            op(("st_o", j, None), [("cp_o", j, 0), ("cp_o", j, 1)], lambda j=j: st_o(j, None))
+        for tok0, n in BLOCKS:
+            op(("st_p", tok0, n), [("q_p", j, og) for j in range(tok0 // P, (tok0 + n) // P) for og in range(2)],
+               lambda tok0=tok0, n=n: nc.sync.dma_start(out=words_out[:, :, tok0: tok0 + n],
+                                                        in_=p_codes[:, :, tok0: tok0 + n].bitcast(I32)))
+        for q in range(4):
+            op(("st_s", q), [("q_p", j, og) for j in range(4) for og in range(2)], lambda q=q: st_s(q))
+
+        queues = [sync_q, pool_q, act_q, pe_q, vec_q]
+        heads = [0] * len(queues)
+        done = set()
+        while any(heads[i] < len(q) for i, q in enumerate(queues)):
+            moved = False
+            for i, q in enumerate(queues):
+                while heads[i] < len(q):
+                    name = q[heads[i]]
+                    needs, fn = ops[name]
+                    if not all(n in done for n in needs + bank_free.get(name, [])):
+                        break
+                    fn()
+                    done.add(name)
+                    heads[i] = heads[i] + 1
+                    moved = True
+            assert moved, [q[heads[i]] for i, q in enumerate(queues) if heads[i] < len(q)]

@@ -17,14 +17,14 @@ ACT = mybir.ActivationFunctionType
 AX = mybir.AxisListType
 
 P = 128
-BLOCKS = [(0, 128), (128, 128), (256, 128), (384, 128)]
-STEPS = [(tok0, n, fg) for tok0, n in BLOCKS for fg in range(2)]
-H_BUFS = 9
+TILES = T // P
+LAST = TILES - 1
+STEPS = 2 * TILES
+XE_BUFS = 7
 W_BUFS = 5
-QP_LAG = 3
-LEAD = 5
-SECOND_PER_UNIT = 1
-PIECES = [0, 0, 0, 1, 2, 3, 4, 5, 6, 6, 7, 7, 8]
+H_BUFS = 9
+WARM_MATMULS = 4
+VECTOR_ADD_FT = 3
 
 
 def tile_batchensemblerankoneexpertmixturemlp_x1_kernel(tc, x, wg, r1, w1, s1, r2, w2, out_0, out_1, out_2):
@@ -37,213 +37,195 @@ def tile_batchensemblerankoneexpertmixturemlp_x1_kernel(tc, x, wg, r1, w1, s1, r
         def tiles(name, count, shape, dtype):
             return [keep.tile(shape, dtype, name="%s%d" % (name, i), align_bytes=64) for i in range(count)]
 
+        def tile(name, shape, dtype):
+            return keep.tile(shape, dtype, name=name, align_bytes=64)
+
         bank = [psum.tile([P, 512], F32, name="bank%d" % i) for i in range(8)]
-        ident, = tiles("ident", 1, [P, P], F32)
+        ident = tile("ident", [P, P], F32)
+        zeros = tile("zeros", [P, 512], BF16)
         warm_in, warm_out = tiles("warm", 2, [P, 1], F32)
-        par_rows = tiles("par_rows", 2, [P, 512], BF16)
-        r1_col, = tiles("r1_col", 1, [P, 8, 2, 2], BF16)
-        sr_col, = tiles("sr_col", 1, [P, 16, 4], F32)
-        wg_sb, = tiles("wg_sb", 1, [P, 2, 4, E], BF16)
+        vec_rows = tiles("vec_rows", 2, [P, 512], BF16)
+        r1_col = tile("r1_col", [P, 8, 2, 2], BF16)
+        sr_col = tile("sr_col", [P, 16, 4], F32)
+        wg_sb = tile("wg_sb", [P, 2, 4, E], BF16)
         x_rows = tiles("x_rows", 4, [P, 2, 512], BF16)
-        x_t, = tiles("x_t", 1, [P, 2, T, 4], BF16)
-        xe = tiles("xe", 7, [P, T, 4], BF16)
+        x_t = tile("x_t", [P, 2, T, 4], BF16)
+        xe = tiles("xe", XE_BUFS, [P, T, 4], BF16)
         xe_codes = tiles("xe_codes", E, [P, 2, T], U32)
         xe_scales = tiles("xe_scales", E, [P, 2, T], U8)
-        w_raw = {}
-        for which in range(2):
-            for g in range(2):
-                for c in range(2):
-                    w_raw[which, g, c], = tiles("w_raw%d%d%d_" % (which, g, c), 1, [P, 4, 512], BF16)
+        w_raw = tiles("w_raw", 4, [P, 4, 1024], BF16)
         w_grouped = tiles("w_grouped", W_BUFS, [P, 512, 4], BF16)
         w_codes = tiles("w_codes", 2, [P, 2, 1024], U32)
         w_scales = tiles("w_scales", 2, [P, 2, 1024], U8)
-        gate_max, gate_sum, gate_inv = tiles("gate_a", 3, [P, 4], F32)
-        gate_d, gate_th, gate_den, gate_rden, gate_ex, gate = tiles("gate_b", 6, [P, 4, E], F32)
+        gate_max, gate_sum, gate_inv = tiles("gate_stat", 3, [P, TILES], F32)
+        gate_d, gate_th, gate_den, gate_rden, gate_ex, gate = tiles("gate_val", 6, [P, TILES, E], F32)
         h = tiles("h", H_BUFS, [P, 512], F32)
-        term1 = tiles("term1_", 3, [P, 512], F32)
-        acc, = tiles("acc", 1, [P, 8, T], F32)
-        term2 = tiles("term2_", 2, [P, 4, 256], F32)
-        term3 = tiles("term3_", 2, [P, 4, 256], F32)
-        part, = tiles("part", 1, [P, 4, 256], F32)
-        m_bf = tiles("m_bf", 2, [P, 256, 4], BF16)
-        m_codes, = tiles("m_codes", 1, [P, 2, T], U32)
-        m_scales, = tiles("m_scales", 1, [P, 2, T], U8)
+        acc = tile("acc", [P, 8, T], F32)
+        term1 = tile("term1", [P, 4, T], F32)
+        term2 = tiles("term2_", 2, [P, 8, P], F32)
+        term3 = tiles("term3_", 2, [P, 4, P], F32)
+        part = tile("part", [P, 8, P], F32)
+        m_bf = tiles("m_bf", 2, [P, 2 * P, 4], BF16)
+        m_codes = tile("m_codes", [P, TILES, 2, P], U32)
+        m_scales = tile("m_scales", [P, TILES, 2, P], U8)
         out_sb = tiles("out_sb", 3, [P, O], F32)
+        early_p = tiles("early_p", 2, [P, P, 4], F32)
         p_bf = tiles("p_bf", 4, [P, P, 4], BF16)
-        p_codes, = tiles("p_codes", 1, [P, 2, T], U32)
-        p_scales, = tiles("p_scales", 1, [P, 2, T], U8)
+        p_codes = tile("p_codes", [P, 2, T], U32)
+        p_scales = tile("p_scales", [P, 2, T], U8)
 
-        ops = {}
+        wide = [("wide", ft, e) for ft in range(8) for e in range(2)]
+        groups = [[2 * j, 2 * j + 1] for j in range(LAST)] + [[STEPS - 2], [STEPS - 1]]
+        narrow = [("narrow", k, 2) for k in groups[0]]
+        for i, ks in enumerate(groups):
+            narrow += [("narrow", k, 3) for k in ks] + [("narrow", k, 2) for nxt in groups[i + 1: i + 2] for k in nxt]
+        units = wide + narrow
 
-        def op(name, needs, fn):
-            ops[name] = (list(needs), fn)
+        def weave(kind, extras):
+            return [name for u in units for name in [(kind, u)] + extras.get(u, [])]
 
-        def quantize(codes, scales, grouped):
-            nc.vector.quantize_mx(out=codes.bitcast(FP8X4), scales=scales, in_=grouped.rearrange("p c t -> p (c t)"))
+        def both(kind, j):
+            return [(kind, j, 0), (kind, j, 1)]
 
-        def mx_group(out, lhs_codes, lhs_scales, lhs_cols, rhs_codes, rhs_scales, rhs_cols, passes=(0, 1)):
-            for g in passes:
-                nc.tensor.matmul_mx(
-                    out=out,
-                    lhsT=lhs_codes[:, g, lhs_cols].bitcast(FP8X4), lhsT_scale=lhs_scales[:, g, lhs_cols],
-                    rhs=rhs_codes[:, g, rhs_cols].bitcast(FP8X4), rhs_scale=rhs_scales[:, g, rhs_cols],
-                    start=(g == 0), stop=(g == 1))
+        def group_of(k):
+            return [ks for ks in groups if k in ks][0]
 
-        w1_chunks = [(0, 0, 0), (0, 1, 0), (0, 0, 1), (0, 1, 1)]
-        w2_chunks = [(1, 0, 0), (1, 1, 0), (1, 0, 1), (1, 1, 1)]
+        sync_q = [("x_load", 0), ("vec_load", 0), ("x_load", 1), ("w_load", 0, 0), ("x_load", 2), ("x_load", 3),
+                  ("w_load", 0, 1), ("w_load", 1, 0), ("w_load", 1, 1)]
+        for j in range(LAST):
+            sync_q += [("st_o", j, 0, 2), ("st_p", j)]
+        sync_q += [("st_o", LAST, 0, 1), ("st_o", LAST, 1, 2), ("st_p", LAST), ("st_s", 0), ("st_s", 1)]
 
-        def step_banks(k):
-            return STEPS[k][1] // P
+        pool_q = [("zeros",), ("ident",), ("wg_load",), ("vec_load", 1), ("vec_load", 2),
+                  ("il", (0, 0, 0), 0, 4), ("il", (0, 1, 0), 0, 4)]
+        pool_q += [("add1", ft) for ft in range(8) if ft != VECTOR_ADD_FT] + [("add2", ks[-1]) for ks in groups[:-1]]
 
-        def a_units():
-            return [("A", ft, e) for ft in range(8) for e in range(2)]
+        vec_q = [("memset",), ("vec_copy", 0)] + [("mult", e, b) for b in range(2) for e in range(E)]
+        vec_q += [("mult", 0, 2), ("q_w", (0, 0, 0)), ("mult", 1, 2), ("mult", 0, 3), ("mult", 1, 3), ("mult", 2, 2), ("mult", 2, 3)]
+        vec_q += [("gate", 0), ("vec_copy", 1), ("gate", 1), ("q_xe", 0, 0), ("q_xe", 0, 1), ("q_w", (0, 1, 0))]
+        between = [("q_xe", 1, 0), ("q_xe", 1, 1), ("q_w", (0, 0, 1)), ("q_xe", 2, 0), ("q_xe", 3, 0), ("q_w", (0, 1, 1))]
+        for step, name in zip(range(3, 9), between):
+            vec_q += [("gate", step), name]
+        vec_q += [("q_xe", 2, 1)]
+        vec_q += weave("term", {
+            ("wide", 0, 1): [("q_w", (1, 0, 0))],
+            ("wide", 2, 1): [("mult", 3, 2)],
+            ("wide", 4, 1): [("add1", VECTOR_ADD_FT), ("mult", 3, 3)],
+            ("wide", 5, 1): [("q_xe", 3, 1)],
+            ("narrow", 1, 2): [("q_w", (1, 0, 1))],
+            ("narrow", 3, 2): [("final", 0), ("final", 1), ("q_w", (1, 1, 0))],
+            ("narrow", 5, 2): [("q_m", 1), ("final", 2), ("final", 3), ("q_w", (1, 1, 1))],
+            ("narrow", 6, 2): [("q_m", 3), ("final", 4), ("final", 5)],
+            ("narrow", 7, 2): [("q_m", 5)] + both("q_p", 0) + [("q_p", 1, 0), ("final", 6)],
+            ("narrow", 7, 3): [("add2", 7), ("q_m", 6), ("q_p", 1, 1), ("final", 7)] + both("q_p", 2) + [("q_m", 7)],
+        })
+        vec_q += both("cp_p", LAST) + both("q_p", LAST)
 
-        def b_units(k, e):
-            return [("B", k, e, i) for i in range(step_banks(k))]
-
-        b_order = b_units(0, 2)
-        for k in range(len(STEPS)):
-            b_order = b_order + b_units(k, 3) + (b_units(k + 1, 2) if k + 1 < len(STEPS) else [])
-        units = a_units() + b_order
-
-        def gelus(us):
-            return [("gelu", u) for u in us]
-
-        def stts(us):
-            return [("stt", u) for u in us]
-
-        def mms(us):
-            return [("mm", u) for u in us]
-
-        au = a_units()
-        n_steps = len(STEPS)
-        tiles_after = {k: list(range(tok0 // P, (tok0 + n) // P)) for k, (tok0, n, fg) in enumerate(STEPS) if fg == 1}
-        last_j = T // P - 1
-
-        sync_q = [("x_load", 0), ("par_load", 0)] + [("x_load", b) for b in range(1, 4)] + [("w_load", c) for c in w1_chunks + w2_chunks]
-        for tok0, n in BLOCKS[:-1]:
-            sync_q += [("st_o", j, None) for j in range(tok0 // P, (tok0 + n) // P)] + [("st_p", tok0, n)]
-        sync_q += [("st_o", last_j, 0), ("st_o", last_j, 1), ("st_p",) + BLOCKS[-1], ("st_s", 0), ("st_s", 1)]
-
-        pool_q = [("ident",), ("wg_load",), ("par_load", 1), ("par_load", 2), ("il", w1_chunks[0], 0, 4), ("il", w1_chunks[2], 0, 4)]
-        pool_q += [("add1", ft) for ft in range(8)] + [("add2", k) for k in range(n_steps)]
-
-        vec_q = [("memset",), ("par_copy", 0)]
-        vec_q += [("mult", e, b) for b in range(2) for e in range(4)]
-        vec_q += [("mult", e, 2) for e in range(3)] + [("par_copy", 1)]
-        vec_q += [("mult", 0, 3), ("mult", 1, 3), ("mult", 2, 3)]
-        vec_q += [("q_xe", 0, 0), ("gate", 0), ("q_xe", 0, 1), ("gate", 1), ("q_w", w1_chunks[0]), ("q_w", w1_chunks[1]), ("gate", 3),
-                  ("q_xe", 1, 0), ("gate", 4), ("q_xe", 1, 1), ("gate", 5), ("q_w", w1_chunks[2]), ("gate", 6),
-                  ("q_w", w1_chunks[3]), ("gate", 7), ("q_xe", 2, 0), ("gate", 8), ("q_xe", 2, 1), ("q_xe", 3, 0), ("q_w", w2_chunks[0])]
-        a_before = {1: [("mult", 3, 2)], 2: [("mult", 3, 3)]}
-        a_after = {3: [("q_xe", 3, 1)], 4: [("q_w", w2_chunks[1])], 6: [("q_w", w2_chunks[2])]}
-        for ft in range(8):
-            vec_q += a_before.get(ft, []) + stts(au[2 * ft: 2 * ft + 2]) + a_after.get(ft, [])
-        vec_q += stts(b_units(0, 2))
-        b_port = {0: [("q_w", w2_chunks[3])]}
-        vec_copies = [("cp_p", last_j - 1, 0), ("cp_p", last_j, 1), ("cp_o", last_j, 1)]
-        for k in range(n_steps):
-            vec_q += stts(b_units(k, 3)) + (stts(b_units(k + 1, 2)) if k + 1 < n_steps else [])
-            if k == n_steps - 1:
-                vec_q += [("cp_p", last_j - 1, 0)]
-            vec_q += ([("q_m", k - 1)] if k else []) + b_port.get(k, [])
-            if k < n_steps - 1:
-                vec_q += [("q_p", j, og) for j in tiles_after.get(k - QP_LAG, []) for og in range(2)]
-            vec_q += [("final", k)]
-        late = [("q_p", j, og) for j in range(last_j) for og in range(2) if ("q_p", j, og) not in vec_q]
-        vec_q += late[:1] + [("q_m", n_steps - 1)] + late[1:]
-        vec_q += [("cp_o", last_j, 1), ("cp_p", last_j, 1), ("q_p", last_j, 0), ("q_p", last_j, 1)]
-
-        def vec_position(k):
-            return sum(1 for name in vec_q[: vec_q.index(("q_m", k))] if name[0] == "stt" and name[1][0] == "B")
-
-        second_at = {}
-        for k, js in tiles_after.items():
-            at = min(vec_position(k) + LEAD, len(b_order))
-            todo = [(kind, j, og) for kind in ("op" if k == n_steps - 1 else "po") for j in js for og in range(2)]
-            for i, item in enumerate(todo):
-                second_at.setdefault(min(at + i // SECOND_PER_UNIT, len(b_order)), []).append(item)
-
-        act_q = [("warm",)]
-        act_q += [("x_copy", 1), ("x_copy", 0), ("x_copy", 2), ("x_copy", 3)]
-        act_q += [("il", w1_chunks[1], 0, 4), ("il", w1_chunks[3], 0, 4), ("il", w2_chunks[0], 0, 2), ("gate", 2)]
-        pieces = [("il", c, q, q + 1) for c in w2_chunks[2:] for q in range(4)]
-        act_q += [("il", w2_chunks[0], 2, 4), ("il", w2_chunks[1], 0, 4)]
-        for ft in range(8):
-            act_q += pieces[PIECES[ft]: PIECES[ft + 1]] + gelus(au[2 * ft: 2 * ft + 2])
-        pe_q = [("par_turn", 0), ("x_turn", 0), ("x_turn", 1), ("x_turn", 2), ("x_turn", 3), ("par_turn", 1), ("logits",)]
-        pe_q += mms(au[0:4]) + [("spread", 0), ("spread", 1)] + mms(au[4:12]) + [("spread", 2), ("spread", 3)] + mms(au[12:])
-        for i in range(len(b_order) + 1):
-            pe_q += [("mm_" + kind, j, og) for kind, j, og in second_at.get(i, [])] + mms(b_order[i: i + 1])
-            act_q += [("cp_" + kind, j, og) for kind, j, og in second_at.get(i - 1, []) if ("cp_" + kind, j, og) not in vec_copies]
-            act_q += pieces[PIECES[8 + min(i, len(PIECES) - 9)]: PIECES[8 + min(i + 1, len(PIECES) - 9)]] + gelus(b_order[i: i + 1])
-        at = pe_q.index(("mm_o", last_j, 0))
-        pe_q = pe_q[:at] + [("mm_early", last_j, 0), ("mm_early", last_j, 1)] + pe_q[at:]
-        act_q += [("cp_" + kind, j, og) for kind, j, og in second_at[len(b_order)] if ("cp_" + kind, j, og) not in vec_copies]
+        act_q = [("warm",), ("x_copy", 1), ("il", (0, 0, 1), 0, 2), ("x_copy", 0), ("x_copy", 2), ("x_copy", 3),
+                 ("il", (0, 0, 1), 2, 4), ("il", (0, 1, 1), 0, 4), ("gate", 2), ("il", (1, 0, 0), 0, 4), ("il", (1, 0, 1), 0, 4)]
+        act_q += weave("gelu", {
+            ("narrow", 0, 2): [("il", (1, 1, 0), 0, 4)],
+            ("narrow", 1, 3): [("il", (1, 1, 1), 0, 1)],
+            ("narrow", 2, 3): [("il", (1, 1, 1), 1, 2)],
+            ("narrow", 5, 3): [("il", (1, 1, 1), 2, 4)],
+            ("narrow", 7, 2): both("cp_p", 0) + both("cp_o", 0) + both("cp_p", 1),
+            ("narrow", 7, 3): both("cp_o", 1) + both("cp_p", 2) + both("cp_o", 2) + both("cp_e", LAST) + both("cp_o", LAST),
+        })
         act_q += [("st_s", 2), ("st_s", 3)]
 
-        bank_of = {("par_turn", 0): 6, ("par_turn", 1): 6, ("logits",): 7, ("spread", 0): 4, ("spread", 1): 5, ("spread", 2): 2, ("spread", 3): 3}
+        pe_q = [("pe_warm",), ("vec_turn", 0)] + [("x_turn", b) for b in range(4)] + [("vec_turn", 1), ("logits",)]
+        pe_q += weave("mm", {
+            ("wide", 1, 1): [("spread", 0), ("spread", 1)],
+            ("narrow", 0, 2): [("spread", 2), ("spread", 3)],
+            ("narrow", 7, 2): [("mm_p", 0, 0)],
+            ("narrow", 7, 3): [("mm_p", 0, 1)] + both("mm_o", 0),
+        })
+        for j in range(1, LAST):
+            pe_q += both("mm_p", j) + both("mm_o", j)
+        pe_q += both("mm_e", LAST) + both("mm_open", LAST) + both("mm_o", LAST) + both("mm_p", LAST)
+
+        bank_of = {("pe_warm",): 5, ("vec_turn", 0): 6, ("vec_turn", 1): 6, ("logits",): 7,
+                   ("spread", 0): 4, ("spread", 1): 5, ("spread", 2): 2, ("spread", 3): 3}
         for b in range(4):
             bank_of["x_turn", b] = b
-        ring_a, ring_b, ring_out = [6, 7, 0, 1], [6, 7, 0], [1, 4, 5]
-        for i, u in enumerate(au):
-            bank_of["mm", u] = ring_a[i % 4]
-        for i, u in enumerate(b_order):
-            bank_of["mm", u] = ring_b[i % 3]
-        second = [name for name in pe_q if name[0] in ("mm_p", "mm_o")]
-        for i, name in enumerate(second[:-4]):
-            bank_of[name] = ring_out[i % 3]
-        for name, b in zip(second[-4:], [6, 7, 0, 2]):
-            bank_of[name] = b
+        for i, u in enumerate(wide):
+            bank_of["mm", u] = [6, 7, 0, 1][i % 4]
+        for i, u in enumerate(narrow):
+            bank_of["mm", u] = [6, 7, 0][i % 3]
+        for i, name in enumerate(name for j in range(LAST) for name in both("mm_p", j) + both("mm_o", j)):
+            bank_of[name] = [1, 4, 5][i % 3]
         for og in range(2):
-            bank_of["mm_early", last_j, og] = bank_of["mm_o", last_j, og]
+            bank_of["mm_open", LAST, og] = bank_of["mm_o", LAST, og] = [6, 7][og]
+            bank_of["mm_e", LAST, og] = bank_of["mm_p", LAST, og] = [0, 2][og]
 
         def readers(name):
             kind = name[0]
             if kind == "x_turn":
                 return [("x_copy", name[1])] + [("mult", e, name[1]) for e in range(E)]
-            if kind == "par_turn":
-                return [("par_copy", name[1])]
+            if kind == "vec_turn":
+                return [("vec_copy", name[1])]
             if kind == "logits":
                 return [("gate", 0), ("gate", 1)]
             if kind == "spread":
-                return [("stt", u) for u in units if u[2] == name[1]]
-            if kind == "mm_early":
-                return []
+                return [("term", u) for u in units if u[2] == name[1]]
             if kind == "mm":
                 return [("gelu", name[1])]
-            return [("cp_p" if kind == "mm_p" else "cp_o",) + name[1:]]
+            if kind in ("pe_warm", "mm_open"):
+                return []
+            return [({"mm_p": "cp_p", "mm_o": "cp_o", "mm_e": "cp_e"}[kind],) + name[1:]]
 
-        bank_free = {}
-        holder = {}
-        for name in pe_q:
-            b = bank_of[name]
-            bank_free[name] = readers(holder[b]) if b in holder else []
-            holder[b] = name
+        ops = {}
+
+        def op(name, needs, fn):
+            ops[name] = (needs, fn)
+
+        def quantize(codes, scales, grouped):
+            nc.vector.quantize_mx(out=codes.bitcast(FP8X4), scales=scales, in_=grouped.rearrange("p c t -> p (c t)"))
+
+        def mx_pass(out, g, lhs, rhs, start, stop):
+            nc.tensor.matmul_mx(
+                out=out,
+                lhsT=lhs[0][:, g, lhs[2]].bitcast(FP8X4), lhsT_scale=lhs[1][:, g, lhs[2]],
+                rhs=rhs[0][:, g, rhs[2]].bitcast(FP8X4), rhs_scale=rhs[1][:, g, rhs[2]],
+                start=start, stop=stop)
 
         def memsets():
-            nc.vector.memset(par_rows[0][:].bitcast(I32), 0)
-            nc.vector.memset(par_rows[1][:].bitcast(I32), 0)
+            nc.vector.memset(vec_rows[0][:].bitcast(I32), 0)
+            nc.vector.memset(vec_rows[1][:].bitcast(I32), 0)
             nc.vector.memset(warm_in[:], 0.0)
 
+        def pe_warm():
+            for i in range(WARM_MATMULS):
+                nc.tensor.matmul(bank[5][:], lhsT=zeros[:, 0:P], rhs=zeros[:], start=True, stop=True)
+
+        def vec_load(i):
+            rows = (r1, s1, r2)[i].rearrange("e (g k) -> (e g) k", g=2)
+            if i == 0:
+                nc.sync.dma_start(out=vec_rows[0][0:8, :], in_=rows)
+            else:
+                nc.gpsimd.dma_start(out=vec_rows[1][8 * i - 8: 8 * i, :], in_=rows)
+
+        def x_load(b):
+            g, half = divmod(b, 2)
+            rows = x[256 * half: 256 * half + 256, 512 * g: 512 * g + 512]
+            nc.sync.dma_start(out=x_rows[b][:], in_=rows.rearrange("(j p) d -> p j d", p=P))
+
+        def w_load(which, g):
+            rows = (w1, w2)[which][512 * g: 512 * g + 512, :]
+            nc.sync.dma_start(out=w_raw[2 * which + g][:], in_=rows.rearrange("(p t) c -> p t c", t=4))
+
         op(("memset",), [], memsets)
+        op(("zeros",), [], lambda: nc.gpsimd.memset(zeros[:].bitcast(I32), 0))
+        op(("pe_warm",), [("zeros",)], pe_warm)
         op(("ident",), [], lambda: make_identity(nc, ident[:]))
         op(("warm",), [("memset",)], lambda: nc.scalar.activation(out=warm_out[:], in_=warm_in[:], func=ACT.Gelu))
-        for i, vec in enumerate((r1, s1, r2)):
-            op(("par_load", i), [("memset",)], lambda i=i, vec=vec: (nc.gpsimd if i else nc.sync).dma_start(
-                out=par_rows[min(i, 1)][8 * (i // 2): 8 * (i // 2) + 8, :], in_=vec.rearrange("e (g k) -> (e g) k", g=2)))
         op(("wg_load",), [], lambda: nc.gpsimd.dma_start(
             out=wg_sb[:].rearrange("p g t e -> p g (t e)"), in_=wg.rearrange("(g p t) e -> p g (t e)", g=2, t=4)))
+        for i in range(3):
+            op(("vec_load", i), [("memset",)], lambda i=i: vec_load(i))
         for b in range(4):
-            g, half = divmod(b, 2)
-            op(("x_load", b), [], lambda b=b, g=g, half=half: nc.sync.dma_start(
-                out=x_rows[b][:],
-                in_=x[256 * half: 256 * half + 256, 512 * g: 512 * g + 512].rearrange("(j p) d -> p j d", p=P)))
-        for chunk in w1_chunks + w2_chunks:
-            which, g, c = chunk
-            op(("w_load", chunk), [], lambda chunk=chunk, which=which, g=g, c=c: nc.sync.dma_start(
-                out=w_raw[chunk][:],
-                in_=(w1, w2)[which][512 * g: 512 * g + 512, 512 * c: 512 * c + 512].rearrange("(p j) f -> p j f", j=4)))
+            op(("x_load", b), [], lambda b=b: x_load(b))
+            op(("w_load",) + divmod(b, 2), [], lambda b=b: w_load(*divmod(b, 2)))
 
         def x_turn(b):
             words = x_rows[b][:].bitcast(F32)
@@ -251,12 +233,12 @@ def tile_batchensemblerankoneexpertmixturemlp_x1_kernel(tc, x, wg, r1, w1, s1, r
                 for u in range(2):
                     nc.tensor.transpose(bank[b][:, 256 * u + P * j: 256 * u + P * j + P], words[:, j, u:256:2], ident[:])
 
-        def par_turn(i):
-            words = par_rows[i][:].bitcast(F32)
+        def vec_turn(i):
+            words = vec_rows[i][:].bitcast(F32)
             for u in range(2):
                 nc.tensor.transpose(bank[6][:, P * u: P * u + P], words[:, u:256:2], ident[:])
 
-        def par_copy(i):
+        def vec_copy(i):
             cols = bank[6][:, 0:256].bitcast(BF16).rearrange("p (u r c) -> p r u c", u=2, c=2)
             if i == 0:
                 nc.vector.tensor_copy(out=r1_col[:], in_=cols[:, 0:8])
@@ -265,76 +247,78 @@ def tile_batchensemblerankoneexpertmixturemlp_x1_kernel(tc, x, wg, r1, w1, s1, r
 
         def x_copy(b):
             g, half = divmod(b, 2)
-            dst = x_t[:, g, 256 * half: 256 * half + 256, :].rearrange("p k t -> p (k t)").bitcast(F32)
-            nc.scalar.copy(out=dst.rearrange("p (k u) -> p k u", u=2), in_=bank[b][:].rearrange("p (u k) -> p k u", u=2))
+            dst = x_t[:, g, 256 * half: 256 * half + 256, :].rearrange("p n t -> p (n t)").bitcast(F32)
+            nc.scalar.copy(out=dst.rearrange("p (n u) -> p n u", u=2), in_=bank[b][:].rearrange("p (u n) -> p n u", u=2))
 
         def xe_tile(e, g):
-            return xe[(4 * g + e) % 7]
+            return xe[(E * g + e) % XE_BUFS]
 
         def mult(e, b):
             g, half = divmod(b, 2)
             nc.vector.tensor_tensor(
-                out=xe_tile(e, g)[:, 256 * half: 256 * half + 256, :].rearrange("p k (u c) -> p k u c", u=2),
-                in0=bank[b][:].bitcast(BF16).rearrange("p (u k c) -> p k u c", u=2, c=2),
+                out=xe_tile(e, g)[:, 256 * half: 256 * half + 256, :].rearrange("p n (u c) -> p n u c", u=2),
+                in0=bank[b][:].bitcast(BF16).rearrange("p (u n c) -> p n u c", u=2, c=2),
                 in1=r1_col[:, 2 * e + g].unsqueeze(1).to_broadcast([P, 256, 2, 2]),
                 op=ALU.mult)
 
         for b in range(4):
             op(("x_turn", b), [("x_load", b), ("ident",)], lambda b=b: x_turn(b))
-            op(("x_copy", b), [("x_turn", b)] + ([("mult", e, 0) for e in range(E)] if b == 0 else []), lambda b=b: x_copy(b))
+            op(("x_copy", b), [("x_turn", b)] + [("mult", e, 0) for e in range(E) if b == 0], lambda b=b: x_copy(b))
             for e in range(E):
-                needs = [("x_turn", b), ("par_copy", 0)] + ([("x_copy", b)] if b else [])
-                if e == 3 and b >= 2:
-                    needs.append(("q_xe", 0, 0))
-                op(("mult", e, b), needs, lambda e=e, b=b: mult(e, b))
+                needs = [("x_turn", b), ("vec_copy", 0)] + ([("x_copy", b)] if b else [])
+                op(("mult", e, b), needs + ([("q_xe", 0, 0)] if E * (b // 2) + e >= XE_BUFS else []), lambda e=e, b=b: mult(e, b))
+        op(("vec_turn", 0), [("vec_load", 0), ("ident",)], lambda: vec_turn(0))
+        op(("vec_turn", 1), [("vec_load", 1), ("vec_load", 2)], lambda: vec_turn(1))
         for i in range(2):
-            op(("par_turn", i), [("par_load", i), ("par_load", 2 * i), ("ident",)], lambda i=i: par_turn(i))
-            op(("par_copy", i), [("par_turn", i)], lambda i=i: par_copy(i))
+            op(("vec_copy", i), [("vec_turn", i)], lambda i=i: vec_copy(i))
         for e in range(E):
             for g in range(2):
                 op(("q_xe", e, g), [("mult", e, 2 * g), ("mult", e, 2 * g + 1)], lambda e=e, g=g: quantize(
                     xe_codes[e][:, g, :], xe_scales[e][:, g, :], xe_tile(e, g)[:]))
 
-        il_names = [name for name in pool_q + act_q if name[0] == "il"]
-        chunk_order = [name[1] for name in vec_q if name[0] == "q_w"]
+        copies = [name for name in pool_q + act_q if name[0] == "il"]
+        chunks = [name[1] for name in vec_q if name[0] == "q_w"]
 
         def interleave(chunk, q0, q1):
-            dst = w_grouped[chunk_order.index(chunk) % W_BUFS]
+            which, g, group = chunk
+            raw = w_raw[2 * which + g][:, :, 512 * group: 512 * group + 512]
+            dst = w_grouped[chunks.index(chunk) % W_BUFS]
             if ("il", chunk, q0, q1) in pool_q:
                 nc.gpsimd.tensor_scalar(
-                    out=dst[:].rearrange("p (t m) j -> p t m j", t=4),
-                    in0=w_raw[chunk][:].rearrange("p j (m t) -> p t m j", t=4),
+                    out=dst[:].rearrange("p (s c) t -> p s c t", s=4), in0=raw.rearrange("p t (c s) -> p s c t", s=4),
                     scalar1=1.0, scalar2=0.0, op0=ALU.mult, op1=ALU.add)
             else:
                 nc.scalar.copy(
-                    out=dst[:].rearrange("p (t a i) j -> p a t i j", t=4, i=2)[:, 16 * q0: 16 * q1],
-                    in_=w_raw[chunk][:].rearrange("p j (a i t) -> p a t i j", t=4, i=2)[:, 16 * q0: 16 * q1])
+                    out=dst[:].rearrange("p (s a i) t -> p a s i t", s=4, i=2)[:, 16 * q0: 16 * q1],
+                    in_=raw.rearrange("p t (a i s) -> p a s i t", s=4, i=2)[:, 16 * q0: 16 * q1])
 
-        for name in il_names:
-            n = chunk_order.index(name[1])
-            op(name, [("w_load", name[1])] + ([("q_w", chunk_order[n - W_BUFS])] if n >= W_BUFS else []),
+        def q_w(chunk):
+            which, g, group = chunk
+            cols = slice(512 * group, 512 * group + 512)
+            quantize(w_codes[which][:, g, cols], w_scales[which][:, g, cols], w_grouped[chunks.index(chunk) % W_BUFS][:])
+
+        for name in copies:
+            n = chunks.index(name[1])
+            op(name, [("w_load",) + name[1][:2]] + ([("q_w", chunks[n - W_BUFS])] if n >= W_BUFS else []),
                lambda name=name: interleave(*name[1:]))
-        for n, chunk in enumerate(chunk_order):
-            which, g, c = chunk
-            op(("q_w", chunk), [name for name in il_names if name[1] == chunk], lambda n=n, which=which, g=g, c=c: quantize(
-                w_codes[which][:, g, 512 * c: 512 * c + 512], w_scales[which][:, g, 512 * c: 512 * c + 512], w_grouped[n % W_BUFS][:]))
+        for chunk in chunks:
+            op(("q_w", chunk), [name for name in copies if name[1] == chunk], lambda chunk=chunk: q_w(chunk))
 
-        logits_ps = bank[7][:, 0:16].rearrange("p (j e) -> p j e", e=E)
+        logits_ps = bank[7][:, 0: TILES * E].rearrange("p (j e) -> p j e", e=E)
 
         def logits():
-            for j in range(4):
+            for j in range(TILES):
                 for g in range(2):
                     for t in range(4):
                         nc.tensor.matmul(logits_ps[:, j, :], lhsT=x_t[:, g, P * j: P * j + P, t], rhs=wg_sb[:, g, t, :],
                                          start=(g == 0 and t == 0), stop=(g == 1 and t == 3))
 
-        def over_experts(col):
-            return col[:].unsqueeze(2).to_broadcast([P, 4, E])
+        def over_experts(stat):
+            return stat[:].unsqueeze(2).to_broadcast([P, TILES, E])
 
-        def flat(tile):
-            return tile[:].rearrange("p j e -> p (j e)")
+        def flat(val):
+            return val[:].rearrange("p j e -> p (j e)")
 
-        op(("logits",), [("x_copy", b) for b in range(4)] + [("wg_load",)], logits)
         gate_steps = [
             lambda: nc.vector.tensor_reduce(out=gate_max[:], in_=logits_ps, axis=AX.X, op=ALU.max),
             lambda: nc.vector.tensor_tensor(out=gate_d[:], in0=logits_ps, in1=over_experts(gate_max), op=ALU.subtract),
@@ -348,144 +332,171 @@ def tile_batchensemblerankoneexpertmixturemlp_x1_kernel(tc, x, wg, r1, w1, s1, r
             lambda: nc.vector.reciprocal(out=gate_inv[:], in_=gate_sum[:]),
             lambda: nc.vector.tensor_tensor(out=gate[:], in0=gate_ex[:], in1=over_experts(gate_inv), op=ALU.mult),
         ]
-        for i, fn in enumerate(gate_steps):
-            op(("gate", i), [("gate", i - 1) if i else ("logits",)], fn)
 
         def spread(e):
-            for j in range(4):
+            for j in range(TILES):
                 nc.tensor.transpose(bank[bank_of["spread", e]][:, P * j: P * j + P],
                                     gate[:, j, e: e + 1].to_broadcast([P, P]), ident[:])
 
+        op(("logits",), [("x_copy", b) for b in range(4)] + [("wg_load",)], logits)
+        for i, fn in enumerate(gate_steps):
+            op(("gate", i), [("gate", i - 1) if i else ("logits",)], fn)
         for e in range(E):
-            op(("spread", e), [("gate", 8)], lambda e=e: spread(e))
+            op(("spread", e), [("gate", len(gate_steps) - 1)], lambda e=e: spread(e))
 
         def unit_parts(u):
-            if u[0] == "A":
-                return [(u[1], 0, T, 0)]
-            tok0, n, fg = STEPS[u[1]]
-            per_bank = 512 // n
-            return [(4 * fg + per_bank * u[3] + i, tok0, n, n * i) for i in range(per_bank)]
+            if u[0] == "wide":
+                return [(u[1], slice(0, T), slice(0, T))]
+            j, g = divmod(u[1], 2)
+            return [(4 * g + t, slice(P * j, P * j + P), slice(P * t, P * t + P)) for t in range(4)]
 
         def column(row0, e, ft):
             return sr_col[:, row0 + 2 * e + ft // 4, ft % 4: ft % 4 + 1]
 
         def mm(u):
-            e = u[2]
-            for ft, tok0, n, col in unit_parts(u):
-                mx_group(bank[bank_of["mm", u]][:, col: col + n], w_codes[0], w_scales[0], slice(P * ft, P * ft + P),
-                         xe_codes[e], xe_scales[e], slice(tok0, tok0 + n))
+            for ft, tokens, cols in unit_parts(u):
+                for g in range(2):
+                    mx_pass(bank[bank_of["mm", u]][:, cols], g, (w_codes[0], w_scales[0], slice(P * ft, P * ft + P)),
+                            (xe_codes[u[2]], xe_scales[u[2]], tokens), g == 0, g == 1)
 
         def gelu(u):
-            for ft, tok0, n, col in unit_parts(u):
-                nc.scalar.activation(out=h[units.index(u) % H_BUFS][:, col: col + n], in_=bank[bank_of["mm", u]][:, col: col + n],
+            for ft, tokens, cols in unit_parts(u):
+                nc.scalar.activation(out=h[units.index(u) % H_BUFS][:, cols], in_=bank[bank_of["mm", u]][:, cols],
                                      func=ACT.Gelu, scale=column(0, u[2], ft))
 
-        def stt(u):
-            e = u[2]
-            for ft, tok0, n, col in unit_parts(u):
-                if e == 0:
-                    dst = acc[:, ft, :]
-                elif e == 1:
-                    dst = term1[ft % 3][:]
-                else:
-                    dst = (term2, term3)[e - 2][u[1] % 2][:, ft % 4, 0:n]
+        def term(u):
+            k, e = u[1], u[2]
+            for ft, tokens, cols in unit_parts(u):
+                dst = [acc[:, ft, :], term1[:, ft % 4, :], term2[k // 2 % 2][:, ft, :], term3[k % 2][:, ft % 4, :]][e]
                 nc.vector.scalar_tensor_tensor(
-                    out=dst, in0=h[units.index(u) % H_BUFS][:, col: col + n], scalar=column(8, e, ft),
-                    in1=bank[bank_of["spread", e]][:, tok0: tok0 + n], op0=ALU.mult, op1=ALU.mult)
+                    out=dst, in0=h[units.index(u) % H_BUFS][:, cols], scalar=column(8, e, ft),
+                    in1=bank[bank_of["spread", e]][:, tokens], op0=ALU.mult, op1=ALU.mult)
 
         for i, u in enumerate(units):
-            e = u[2]
-            fg = u[1] // 4 if u[0] == "A" else STEPS[u[1]][2]
-            op(("mm", u), [("q_xe", e, 0), ("q_xe", e, 1), ("q_w", (0, 0, fg)), ("q_w", (0, 1, fg))], lambda u=u: mm(u))
-            op(("gelu", u), [("mm", u), ("par_copy", 1)] + ([("stt", units[i - H_BUFS])] if i >= H_BUFS else []), lambda u=u: gelu(u))
+            k, e = u[1], u[2]
+            group = k // 4 if u[0] == "wide" else k % 2
+            op(("mm", u), [("q_xe", e, 0), ("q_xe", e, 1), ("q_w", (0, 0, group)), ("q_w", (0, 1, group))], lambda u=u: mm(u))
+            op(("gelu", u), [("mm", u), ("vec_copy", 1)] + ([("term", units[i - H_BUFS])] if i >= H_BUFS else []), lambda u=u: gelu(u))
             needs = [("gelu", u), ("spread", e)]
-            if e == 1 and u[1] >= 3:
-                needs.append(("add1", u[1] - 3))
-            if e >= 2 and u[1] >= 2:
-                needs.append(("add2" if e == 2 else "final", u[1] - 2))
-            op(("stt", u), needs, lambda u=u: stt(u))
+            if e == 1 and k >= 4:
+                needs.append(("add1", k - 4))
+            if e == 2 and k >= 4:
+                needs.append(("add2", group_of(k - 4)[-1]))
+            if e == 3 and k >= 2:
+                needs.append(("final", k - 2))
+            op(("term", u), needs, lambda u=u: term(u))
 
-        def add2(k):
-            tok0, n, fg = STEPS[k]
-            nc.gpsimd.tensor_tensor(out=part[:, :, 0:n], in0=acc[:, 4 * fg: 4 * fg + 4, tok0: tok0 + n],
-                                    in1=term2[k % 2][:, :, 0:n], op=ALU.add)
+        def adder(name):
+            return nc.vector if name in vec_q else nc.gpsimd
+
+        def part_row(k):
+            return 4 * group_of(k).index(k)
+
+        def add1(ft):
+            adder(("add1", ft)).tensor_tensor(out=acc[:, ft, :], in0=acc[:, ft, :], in1=term1[:, ft % 4, :], op=ALU.add)
+
+        def add2(ks):
+            j, fts = ks[0] // 2, slice(4 * (ks[0] % 2), 4 * (ks[-1] % 2) + 4)
+            adder(("add2", ks[-1])).tensor_tensor(out=part[:, 0: 4 * len(ks), :], in0=acc[:, fts, P * j: P * j + P],
+                                                  in1=term2[j % 2][:, fts, :], op=ALU.add)
 
         def final(k):
-            n = STEPS[k][1]
             nc.vector.tensor_tensor(
-                out=m_bf[k % 2][:, 0:n, :].rearrange("p (c i) t -> p c t i", i=4),
-                in0=part[:, :, 0:n].rearrange("p t (c i) -> p c t i", i=4),
-                in1=term3[k % 2][:, :, 0:n].rearrange("p t (c i) -> p c t i", i=4), op=ALU.add)
+                out=m_bf[k // 2 % 2][:, P * (k % 2): P * (k % 2) + P, :].rearrange("p (c i) t -> p c t i", i=4),
+                in0=part[:, part_row(k): part_row(k) + 4, :].rearrange("p t (c i) -> p c t i", i=4),
+                in1=term3[k % 2][:].rearrange("p t (c i) -> p c t i", i=4), op=ALU.add)
+
+        def q_m(ks):
+            j, g0, g1 = ks[0] // 2, ks[0] % 2, ks[-1] % 2 + 1
+            quantize(m_codes[:, j, g0:g1, :].rearrange("p g n -> p (g n)"), m_scales[:, j, g0:g1, :].rearrange("p g n -> p (g n)"),
+                     m_bf[j % 2][:, P * g0: P * g1, :])
 
         for ft in range(8):
-            op(("add1", ft), stts(au[2 * ft: 2 * ft + 2]), lambda ft=ft: nc.gpsimd.tensor_tensor(
-                out=acc[:, ft, :], in0=acc[:, ft, :], in1=term1[ft % 3][:], op=ALU.add))
-        for k, (tok0, n, fg) in enumerate(STEPS):
-            op(("add2", k), stts(b_units(k, 2)) + [("add1", 7)] + ([("final", k - 1)] if k else []), lambda k=k: add2(k))
-            op(("final", k), stts(b_units(k, 3)) + [("add2", k)] + ([("q_m", k - 2)] if k >= 2 else []), lambda k=k: final(k))
-            op(("q_m", k), [("final", k)], lambda k=k, tok0=tok0, n=n, fg=fg: quantize(
-                m_codes[:, fg, tok0: tok0 + n], m_scales[:, fg, tok0: tok0 + n], m_bf[k % 2][:, 0:n, :]))
+            op(("add1", ft), [("term", ("wide", ft, e)) for e in range(2)], lambda ft=ft: add1(ft))
+        for i, ks in enumerate(groups):
+            op(("add2", ks[-1]), [("term", ("narrow", k, 2)) for k in ks] + [("add1", ft) for ft in range(8)]
+               + [("final", k) for k in (groups[i - 1] if i else [])], lambda ks=ks: add2(ks))
+            op(("q_m", ks[-1]), [("final", k) for k in ks], lambda ks=ks: q_m(ks))
+            for k in ks:
+                op(("final", k), [("term", ("narrow", k, 3)), ("add2", ks[-1])]
+                   + ([("q_m", group_of(k - 4)[-1])] if k >= 4 else []), lambda k=k: final(k))
 
-        def mm_p(j, og):
+        def m_operand(j):
+            return (m_codes[:, j], m_scales[:, j], slice(0, P))
+
+        def mm_p(j, og, passes):
             for t in range(4):
-                c0 = 512 * og + P * t
-                mx_group(bank[bank_of["mm_p", j, og]][:, P * t: P * t + P], w_codes[1], w_scales[1], slice(c0, c0 + P),
-                         m_codes, m_scales, slice(P * j, P * j + P))
+                cols = slice(512 * og + P * t, 512 * og + P * t + P)
+                for g in passes:
+                    mx_pass(bank[bank_of["mm_p", j, og]][:, P * t: P * t + P], g, (w_codes[1], w_scales[1], cols), m_operand(j),
+                            g == passes[0], g == passes[-1])
 
         def mm_o(j, og, passes):
-            mx_group(bank[bank_of["mm_o", j, og]][:], m_codes, m_scales, slice(P * j, P * j + P),
-                     w_codes[1], w_scales[1], slice(512 * og, 512 * og + 512), passes)
+            for g in passes:
+                mx_pass(bank[bank_of["mm_o", j, og]][:], g, m_operand(j),
+                        (w_codes[1], w_scales[1], slice(512 * og, 512 * og + 512)), g == 0, g == 1)
 
-        def copy_on(name, out, in_):
-            if name in vec_q:
-                nc.vector.tensor_copy(out=out, in_=in_)
-            else:
-                nc.scalar.copy(out=out, in_=in_)
+        def planes_view(j, og):
+            return bank[bank_of["mm_p", j, og]][:].rearrange("p (t n) -> p n t", t=4)
+
+        def p_tile(j, og):
+            return p_bf[(2 * j + og) % 4]
 
         def cp_p(j, og):
-            copy_on(("cp_p", j, og), p_bf[(2 * j + og) % 4][:],
-                    bank[bank_of["mm_p", j, og]][:].rearrange("p (t k) -> p k t", t=4))
+            if j == LAST:
+                nc.vector.tensor_tensor(out=p_tile(j, og)[:], in0=planes_view(j, og), in1=early_p[og][:], op=ALU.add)
+            else:
+                nc.scalar.copy(out=p_tile(j, og)[:], in_=planes_view(j, og))
 
         def cp_o(j, og):
-            copy_on(("cp_o", j, og), out_sb[j % 3][:, 512 * og: 512 * og + 512].rearrange("p (m t) -> p m t", t=4),
-                    bank[bank_of["mm_o", j, og]][:].rearrange("p (t m) -> p m t", t=4))
+            nc.scalar.copy(out=out_sb[j % 3][:, 512 * og: 512 * og + 512].rearrange("p (c s) -> p c s", s=4),
+                           in_=bank[bank_of["mm_o", j, og]][:].rearrange("p (s c) -> p c s", s=4))
 
-        def st_o(j, og):
-            cols = slice(0, O) if og is None else slice(512 * og, 512 * og + 512)
-            nc.sync.dma_start(out=out_0[P * j: P * j + P, cols], in_=out_sb[j % 3][:, cols])
+        def st_o(j, og0, og1):
+            nc.sync.dma_start(out=out_0[P * j: P * j + P, 512 * og0: 512 * og1], in_=out_sb[j % 3][:, 512 * og0: 512 * og1])
 
         words_out = out_1.rearrange("g p m t -> p g (m t)").bitcast(I32)
         scales_out = out_2.rearrange("g q m -> q g m").bitcast(I32)
+
+        def st_p(j):
+            nc.sync.dma_start(out=words_out[:, :, P * j: P * j + P], in_=p_codes[:, :, P * j: P * j + P].bitcast(I32))
 
         def st_s(q):
             engine = nc.sync if ("st_s", q) in sync_q else nc.scalar
             engine.dma_start(out=scales_out[4 * q: 4 * q + 4], in_=p_scales[32 * q: 32 * q + 4].bitcast(I32))
 
-        for j in range(4):
-            last = max(k for k, (tok0, n, fg) in enumerate(STEPS) if tok0 <= P * j)
-            ready = [("q_m", last - 1), ("q_m", last)] + [("q_w", c) for c in w2_chunks]
+        w2_ready = [("q_w", chunk) for chunk in chunks if chunk[0] == 1]
+        for j in range(TILES):
+            passes = [1] if j == LAST else [0, 1]
             for og in range(2):
-                op(("mm_p", j, og), ready, lambda j=j, og=og: mm_p(j, og))
-                op(("mm_o", j, og), ready, lambda j=j, og=og: mm_o(j, og, (1,) if j == last_j else (0, 1)))
-                op(("mm_early", j, og), ready[:1] + ready[2:], lambda j=j, og=og: mm_o(j, og, (0,)))
+                op(("mm_p", j, og), w2_ready + [("q_m", 2 * j + 1)], lambda j=j, og=og, passes=passes: mm_p(j, og, passes))
+                op(("mm_o", j, og), w2_ready + [("q_m", 2 * j + 1)], lambda j=j, og=og, passes=passes: mm_o(j, og, passes))
                 op(("cp_p", j, og), [("mm_p", j, og)] + ([("q_p", j - 2, og)] if j >= 2 else []), lambda j=j, og=og: cp_p(j, og))
-                op(("cp_o", j, og), [("mm_o", j, og)] + ([("st_o", 0, None)] if j == 3 else []), lambda j=j, og=og: cp_o(j, og))
+                op(("cp_o", j, og), [("mm_o", j, og)] + ([("st_o", j - 3, 0, 2)] if j >= 3 else []), lambda j=j, og=og: cp_o(j, og))
                 op(("q_p", j, og), [("cp_p", j, og)], lambda j=j, og=og: quantize(
-                    p_codes[:, og, P * j: P * j + P], p_scales[:, og, P * j: P * j + P], p_bf[(2 * j + og) % 4][:]))
-                op(("st_o", j, og), [("cp_o", j, og)], lambda j=j, og=og: st_o(j, og))
-            op(("st_o", j, None), [("cp_o", j, 0), ("cp_o", j, 1)], lambda j=j: st_o(j, None))
-        for tok0, n in BLOCKS:
-            op(("st_p", tok0, n), [("q_p", j, og) for j in range(tok0 // P, (tok0 + n) // P) for og in range(2)],
-               lambda tok0=tok0, n=n: nc.sync.dma_start(out=words_out[:, :, tok0: tok0 + n],
-                                                        in_=p_codes[:, :, tok0: tok0 + n].bitcast(I32)))
+                    p_codes[:, og, P * j: P * j + P], p_scales[:, og, P * j: P * j + P], p_tile(j, og)[:]))
+            op(("st_p", j), both("q_p", j), lambda j=j: st_p(j))
+        for og in range(2):
+            op(("mm_e", LAST, og), [("q_m", 2 * LAST)], lambda og=og: mm_p(LAST, og, [0]))
+            op(("mm_open", LAST, og), [("q_m", 2 * LAST)], lambda og=og: mm_o(LAST, og, [0]))
+            op(("cp_e", LAST, og), [("mm_e", LAST, og)], lambda og=og: nc.scalar.copy(out=early_p[og][:], in_=planes_view(LAST, og)))
+        for name in sync_q:
+            if name[0] == "st_o":
+                op(name, [("cp_o", name[1], og) for og in range(name[2], name[3])], lambda name=name: st_o(*name[1:]))
         for q in range(4):
-            op(("st_s", q), [("q_p", j, og) for j in range(4) for og in range(2)], lambda q=q: st_s(q))
+            op(("st_s", q), [name for j in range(TILES) for name in both("q_p", j)], lambda q=q: st_s(q))
+
+        bank_free = {}
+        holder = {}
+        for name in pe_q:
+            bank_free[name] = readers(holder[bank_of[name]]) if bank_of[name] in holder else []
+            holder[bank_of[name]] = name
 
         queues = [sync_q, pool_q, act_q, pe_q, vec_q]
         heads = [0] * len(queues)
         done = set()
         while any(heads[i] < len(q) for i, q in enumerate(queues)):
-            moved = False
+            written = len(done)
             for i, q in enumerate(queues):
                 while heads[i] < len(q):
                     name = q[heads[i]]
@@ -495,5 +506,4 @@ def tile_batchensemblerankoneexpertmixturemlp_x1_kernel(tc, x, wg, r1, w1, s1, r
                     fn()
                     done.add(name)
                     heads[i] = heads[i] + 1
-                    moved = True
-            assert moved, [q[heads[i]] for i, q in enumerate(queues) if heads[i] < len(q)]
+            assert len(done) > written

@@ -97,11 +97,12 @@ def tile_batchensemblerankoneexpertmixturemlp_x1_kernel(tc, x, wg, r1, w1, s1, r
         sync_q += [("st_o", LAST, 0, 1), ("st_o", LAST, 1, 2), ("st_p", LAST), ("st_s", 0), ("st_s", 1)]
 
         pool_q = [("zeros",), ("ident",), ("wg_load",), ("vec_load", 1), ("vec_load", 2),
-                  ("il", (0, 0, 0), 0, 4), ("il", (0, 1, 0), 0, 4)]
+                  ("il", (0, 0, 0), 0, 4)]
         pool_q += [("add1", ft) for ft in range(8) if ft != VECTOR_ADD_FT] + [("add2", ks[-1]) for ks in groups[:-1]]
 
         vec_q = [("memset",), ("vec_copy", 0)] + [("mult", e, b) for b in range(2) for e in range(E)]
-        vec_q += [("mult", 0, 2), ("q_w", (0, 0, 0)), ("mult", 1, 2), ("mult", 0, 3), ("mult", 1, 3), ("mult", 2, 2), ("mult", 2, 3)]
+        vec_q += [("mult", 0, 2), ("mult", 1, 2), ("mult", 0, 3), ("mult", 1, 3), ("mult", 2, 2), ("mult", 2, 3)]
+        vec_q += [("il", (0, 1, 0), 0, 4), ("q_w", (0, 0, 0))]
         vec_q += [("gate", 0), ("vec_copy", 1), ("gate", 1), ("q_xe", 0, 0), ("q_xe", 0, 1), ("q_w", (0, 1, 0))]
         between = [("q_xe", 1, 0), ("q_xe", 1, 1), ("q_w", (0, 0, 1)), ("q_xe", 2, 0), ("q_xe", 3, 0), ("q_w", (0, 1, 1))]
         for step, name in zip(range(3, 9), between):
@@ -276,7 +277,7 @@ def tile_batchensemblerankoneexpertmixturemlp_x1_kernel(tc, x, wg, r1, w1, s1, r
                 op(("q_xe", e, g), [("mult", e, 2 * g), ("mult", e, 2 * g + 1)], lambda e=e, g=g: quantize(
                     xe_codes[e][:, g, :], xe_scales[e][:, g, :], xe_tile(e, g)[:]))
 
-        copies = [name for name in pool_q + act_q if name[0] == "il"]
+        copies = [name for name in pool_q + act_q + vec_q if name[0] == "il"]
         chunks = [name[1] for name in vec_q if name[0] == "q_w"]
 
         def interleave(chunk, q0, q1):
@@ -288,7 +289,7 @@ def tile_batchensemblerankoneexpertmixturemlp_x1_kernel(tc, x, wg, r1, w1, s1, r
                     out=dst[:].rearrange("p (s c) t -> p s c t", s=4), in0=raw.rearrange("p t (c s) -> p s c t", s=4),
                     scalar1=1.0, scalar2=0.0, op0=ALU.mult, op1=ALU.add)
             else:
-                nc.scalar.copy(
+                (nc.vector.tensor_copy if ("il", chunk, q0, q1) in vec_q else nc.scalar.copy)(
                     out=dst[:].rearrange("p (s a i) t -> p a s i t", s=4, i=2)[:, 16 * q0: 16 * q1],
                     in_=raw.rearrange("p t (a i s) -> p a s i t", s=4, i=2)[:, 16 * q0: 16 * q1])
 

@@ -20,9 +20,8 @@ P = 128
 TILES = T // P
 LAST = TILES - 1
 STEPS = 2 * TILES
-XE_BUFS = 7
 W_BUFS = 5
-H_BUFS = 9
+H_BUFS = 8
 WARM_MATMULS = 4
 VECTOR_ADD_FT = 3
 
@@ -50,7 +49,7 @@ def tile_batchensemblerankoneexpertmixturemlp_x1_kernel(tc, x, wg, r1, w1, s1, r
         wg_sb = tile("wg_sb", [P, 2, 4, E], BF16)
         x_rows = tiles("x_rows", 4, [P, 2, 512], BF16)
         x_t = tile("x_t", [P, 2, T, 4], BF16)
-        xe = tiles("xe", XE_BUFS, [P, T, 4], BF16)
+        xe = tiles("xe", 2 * E, [P, T, 4], BF16)
         xe_codes = tiles("xe_codes", E, [P, 2, T], U32)
         xe_scales = tiles("xe_scales", E, [P, 2, T], U8)
         w_raw = tiles("w_raw", 4, [P, 4, 1024], BF16)
@@ -90,46 +89,42 @@ def tile_batchensemblerankoneexpertmixturemlp_x1_kernel(tc, x, wg, r1, w1, s1, r
         def group_of(k):
             return [ks for ks in groups if k in ks][0]
 
-        sync_q = [("x_load", 0), ("vec_load", 0), ("x_load", 1), ("w_load", 0, 0), ("x_load", 2), ("x_load", 3),
-                  ("w_load", 0, 1), ("w_load", 1, 0), ("w_load", 1, 1)]
+        sync_q = [("x_load", 0), ("vec_load", 0), ("w_load", 0, 0, 0, 1), ("x_load", 1), ("w_load", 0, 0, 1, 2), ("x_load", 2), ("x_load", 3),
+                  ("w_load", 0, 1, 0, 2), ("w_load", 1, 0, 0, 2), ("w_load", 1, 1, 0, 2)]
         for j in range(LAST):
             sync_q += [("st_o", j, 0, 2), ("st_p", j)]
         sync_q += [("st_o", LAST, 0, 1), ("st_o", LAST, 1, 2), ("st_p", LAST), ("st_s", 0), ("st_s", 1)]
 
         pool_q = [("zeros",), ("ident",), ("wg_load",), ("vec_load", 1), ("vec_load", 2),
-                  ("il", (0, 0, 0), 0, 4)]
+                  ("il", (0, 0, 0), 0, 4), ("il", (0, 1, 1), 0, 3)]
         pool_q += [("add1", ft) for ft in range(8) if ft != VECTOR_ADD_FT] + [("add2", ks[-1]) for ks in groups[:-1]]
 
         vec_q = [("memset",), ("vec_copy", 0)] + [("mult", e, b) for b in range(2) for e in range(E)]
-        vec_q += [("mult", 0, 2), ("mult", 1, 2), ("mult", 0, 3), ("mult", 1, 3), ("mult", 2, 2), ("mult", 2, 3)]
-        vec_q += [("il", (0, 1, 0), 0, 4), ("q_w", (0, 0, 0))]
-        vec_q += [("gate", 0), ("vec_copy", 1), ("gate", 1), ("q_xe", 0, 0), ("q_xe", 0, 1), ("q_w", (0, 1, 0))]
-        between = [("q_xe", 1, 0), ("q_xe", 1, 1), ("q_w", (0, 0, 1)), ("q_xe", 2, 0), ("q_xe", 3, 0), ("q_w", (0, 1, 1))]
+        vec_q += [("mult", e, b) for pair in range(2) for b in (2, 3) for e in (2 * pair, 2 * pair + 1)]
+        vec_q += [("gate", 0), ("vec_copy", 1), ("il", (0, 1, 0), 0, 3), ("gate", 1), ("q_w", (0, 0, 0)), ("q_xe", 0, 0)]
+        between = [("q_w", (0, 1, 0)), ("q_xe", 0, 1), ("q_xe", 1, 0), ("q_xe", 1, 1), ("q_w", (0, 0, 1)), ("q_w", (0, 1, 1))]
         for step, name in zip(range(3, 9), between):
-            vec_q += [("gate", step), name]
-        vec_q += [("q_xe", 2, 1)]
+            vec_q += [name, ("gate", step)]
+        vec_q += [("q_w", (1, 0, 0)), ("q_w", (1, 0, 1))] + both("q_xe", 2) + both("q_xe", 3)
         vec_q += weave("term", {
-            ("wide", 0, 1): [("q_w", (1, 0, 0))],
-            ("wide", 2, 1): [("mult", 3, 2)],
-            ("wide", 4, 1): [("add1", VECTOR_ADD_FT), ("mult", 3, 3)],
-            ("wide", 5, 1): [("q_xe", 3, 1)],
-            ("narrow", 1, 2): [("q_w", (1, 0, 1))],
-            ("narrow", 3, 2): [("final", 0), ("final", 1), ("q_w", (1, 1, 0))],
-            ("narrow", 5, 2): [("q_m", 1), ("final", 2), ("final", 3), ("q_w", (1, 1, 1))],
-            ("narrow", 6, 2): [("q_m", 3), ("final", 4), ("final", 5)],
+            ("wide", 4, 1): [("add1", VECTOR_ADD_FT)],
+            ("narrow", 1, 2): [("q_w", (1, 1, 0))],
+            ("narrow", 3, 2): [("final", 0), ("final", 1)],
+            ("narrow", 5, 2): [("q_m", 1), ("q_w", (1, 1, 1)), ("final", 2), ("final", 3)],
+            ("narrow", 6, 2): [("cp_p", 0, 0), ("q_m", 3), ("final", 4), ("final", 5)],
             ("narrow", 7, 2): [("q_m", 5)] + both("q_p", 0) + [("q_p", 1, 0), ("final", 6)],
             ("narrow", 7, 3): [("add2", 7), ("q_m", 6), ("q_p", 1, 1), ("final", 7)] + both("q_p", 2) + [("q_m", 7)],
         })
         vec_q += both("cp_p", LAST) + both("q_p", LAST)
 
-        act_q = [("warm",), ("x_copy", 1), ("il", (0, 0, 1), 0, 2), ("x_copy", 0), ("x_copy", 2), ("x_copy", 3),
-                 ("il", (0, 0, 1), 2, 4), ("il", (0, 1, 1), 0, 4), ("gate", 2), ("il", (1, 0, 0), 0, 4), ("il", (1, 0, 1), 0, 4)]
+        act_q = [("warm",), ("il", (0, 0, 1), 0, 2), ("x_copy", 0), ("x_copy", 2), ("x_copy", 3), ("x_copy", 1), ("il", (0, 0, 1), 2, 4),
+                 ("il", (0, 1, 0), 3, 4), ("il", (0, 1, 1), 3, 4), ("il", (1, 0, 0), 0, 4), ("gate", 2), ("il", (1, 0, 1), 0, 4), ("il", (1, 1, 0), 0, 4)]
         act_q += weave("gelu", {
-            ("narrow", 0, 2): [("il", (1, 1, 0), 0, 4)],
-            ("narrow", 1, 3): [("il", (1, 1, 1), 0, 1)],
-            ("narrow", 2, 3): [("il", (1, 1, 1), 1, 2)],
-            ("narrow", 5, 3): [("il", (1, 1, 1), 2, 4)],
-            ("narrow", 7, 2): both("cp_p", 0) + both("cp_o", 0) + both("cp_p", 1),
+            ("wide", 5, 0): [("il", (1, 1, 1), 0, 1)],
+            ("narrow", 0, 2): [("il", (1, 1, 1), 1, 2)],
+            ("narrow", 1, 3): [("il", (1, 1, 1), 2, 3)],
+            ("narrow", 2, 3): [("il", (1, 1, 1), 3, 4)],
+            ("narrow", 7, 2): [("cp_p", 0, 1)] + both("cp_o", 0) + both("cp_p", 1),
             ("narrow", 7, 3): both("cp_o", 1) + both("cp_p", 2) + both("cp_o", 2) + both("cp_e", LAST) + both("cp_o", LAST),
         })
         act_q += [("st_s", 2), ("st_s", 3)]
@@ -211,9 +206,10 @@ def tile_batchensemblerankoneexpertmixturemlp_x1_kernel(tc, x, wg, r1, w1, s1, r
             rows = x[256 * half: 256 * half + 256, 512 * g: 512 * g + 512]
             nc.sync.dma_start(out=x_rows[b][:], in_=rows.rearrange("(j p) d -> p j d", p=P))
 
-        def w_load(which, g):
-            rows = (w1, w2)[which][512 * g: 512 * g + 512, :]
-            nc.sync.dma_start(out=w_raw[2 * which + g][:], in_=rows.rearrange("(p t) c -> p t c", t=4))
+        def w_load(which, g, group0, group1):
+            cols = slice(512 * group0, 512 * group1)
+            rows = (w1, w2)[which][512 * g: 512 * g + 512, cols]
+            nc.sync.dma_start(out=w_raw[2 * which + g][:, :, cols], in_=rows.rearrange("(p t) c -> p t c", t=4))
 
         op(("memset",), [], memsets)
         op(("zeros",), [], lambda: nc.gpsimd.memset(zeros[:].bitcast(I32), 0))
@@ -226,7 +222,9 @@ def tile_batchensemblerankoneexpertmixturemlp_x1_kernel(tc, x, wg, r1, w1, s1, r
             op(("vec_load", i), [("memset",)], lambda i=i: vec_load(i))
         for b in range(4):
             op(("x_load", b), [], lambda b=b: x_load(b))
-            op(("w_load",) + divmod(b, 2), [], lambda b=b: w_load(*divmod(b, 2)))
+        w_loads = [name for name in sync_q if name[0] == "w_load"]
+        for name in w_loads:
+            op(name, [], lambda name=name: w_load(*name[1:]))
 
         def x_turn(b):
             words = x_rows[b][:].bitcast(F32)
@@ -251,23 +249,19 @@ def tile_batchensemblerankoneexpertmixturemlp_x1_kernel(tc, x, wg, r1, w1, s1, r
             dst = x_t[:, g, 256 * half: 256 * half + 256, :].rearrange("p n t -> p (n t)").bitcast(F32)
             nc.scalar.copy(out=dst.rearrange("p (n u) -> p n u", u=2), in_=bank[b][:].rearrange("p (u n) -> p n u", u=2))
 
-        def xe_tile(e, g):
-            return xe[(E * g + e) % XE_BUFS]
-
         def mult(e, b):
             g, half = divmod(b, 2)
             nc.vector.tensor_tensor(
-                out=xe_tile(e, g)[:, 256 * half: 256 * half + 256, :].rearrange("p n (u c) -> p n u c", u=2),
+                out=xe[2 * e + g][:, 256 * half: 256 * half + 256, :].rearrange("p n (u c) -> p n u c", u=2),
                 in0=bank[b][:].bitcast(BF16).rearrange("p (u n c) -> p n u c", u=2, c=2),
                 in1=r1_col[:, 2 * e + g].unsqueeze(1).to_broadcast([P, 256, 2, 2]),
                 op=ALU.mult)
 
         for b in range(4):
             op(("x_turn", b), [("x_load", b), ("ident",)], lambda b=b: x_turn(b))
-            op(("x_copy", b), [("x_turn", b)] + [("mult", e, 0) for e in range(E) if b == 0], lambda b=b: x_copy(b))
+            op(("x_copy", b), [("x_turn", b)] + [("mult", e, b) for e in range(E) if b < 2], lambda b=b: x_copy(b))
             for e in range(E):
-                needs = [("x_turn", b), ("vec_copy", 0)] + ([("x_copy", b)] if b else [])
-                op(("mult", e, b), needs + ([("q_xe", 0, 0)] if E * (b // 2) + e >= XE_BUFS else []), lambda e=e, b=b: mult(e, b))
+                op(("mult", e, b), [("x_turn", b), ("vec_copy", 0)] + ([("x_copy", b)] if b >= 2 else []), lambda e=e, b=b: mult(e, b))
         op(("vec_turn", 0), [("vec_load", 0), ("ident",)], lambda: vec_turn(0))
         op(("vec_turn", 1), [("vec_load", 1), ("vec_load", 2)], lambda: vec_turn(1))
         for i in range(2):
@@ -275,7 +269,7 @@ def tile_batchensemblerankoneexpertmixturemlp_x1_kernel(tc, x, wg, r1, w1, s1, r
         for e in range(E):
             for g in range(2):
                 op(("q_xe", e, g), [("mult", e, 2 * g), ("mult", e, 2 * g + 1)], lambda e=e, g=g: quantize(
-                    xe_codes[e][:, g, :], xe_scales[e][:, g, :], xe_tile(e, g)[:]))
+                    xe_codes[e][:, g, :], xe_scales[e][:, g, :], xe[2 * e + g][:]))
 
         copies = [name for name in pool_q + act_q + vec_q if name[0] == "il"]
         chunks = [name[1] for name in vec_q if name[0] == "q_w"]
@@ -286,7 +280,8 @@ def tile_batchensemblerankoneexpertmixturemlp_x1_kernel(tc, x, wg, r1, w1, s1, r
             dst = w_grouped[chunks.index(chunk) % W_BUFS]
             if ("il", chunk, q0, q1) in pool_q:
                 nc.gpsimd.tensor_scalar(
-                    out=dst[:].rearrange("p (s c) t -> p s c t", s=4), in0=raw.rearrange("p t (c s) -> p s c t", s=4),
+                    out=dst[:].rearrange("p (s c) t -> p s c t", s=4)[:, :, 32 * q0: 32 * q1],
+                    in0=raw.rearrange("p t (c s) -> p s c t", s=4)[:, :, 32 * q0: 32 * q1],
                     scalar1=1.0, scalar2=0.0, op0=ALU.mult, op1=ALU.add)
             else:
                 (nc.vector.tensor_copy if ("il", chunk, q0, q1) in vec_q else nc.scalar.copy)(
@@ -300,7 +295,7 @@ def tile_batchensemblerankoneexpertmixturemlp_x1_kernel(tc, x, wg, r1, w1, s1, r
 
         for name in copies:
             n = chunks.index(name[1])
-            op(name, [("w_load",) + name[1][:2]] + ([("q_w", chunks[n - W_BUFS])] if n >= W_BUFS else []),
+            op(name, [load for load in w_loads if load[1:3] == name[1][:2] and load[3] <= name[1][2] < load[4]] + ([("q_w", chunks[n - W_BUFS])] if n >= W_BUFS else []),
                lambda name=name: interleave(*name[1:]))
         for chunk in chunks:
             op(("q_w", chunk), [name for name in copies if name[1] == chunk], lambda chunk=chunk: q_w(chunk))
@@ -446,6 +441,8 @@ def tile_batchensemblerankoneexpertmixturemlp_x1_kernel(tc, x, wg, r1, w1, s1, r
         def cp_p(j, og):
             if j == LAST:
                 nc.vector.tensor_tensor(out=p_tile(j, og)[:], in0=planes_view(j, og), in1=early_p[og][:], op=ALU.add)
+            elif ("cp_p", j, og) in vec_q:
+                nc.vector.tensor_copy(out=p_tile(j, og)[:], in_=planes_view(j, og))
             else:
                 nc.scalar.copy(out=p_tile(j, og)[:], in_=planes_view(j, og))
 

@@ -96,12 +96,12 @@ def tile_batchensemblerankoneexpertmixturemlp_x1_kernel(tc, x, wg, r1, w1, s1, r
         sync_q += [("st_o", LAST, 0, 1), ("st_o", LAST, 1, 2), ("st_p", LAST), ("st_s", 0), ("st_s", 1)]
 
         pool_q = [("zeros",), ("ident",), ("wg_load",), ("vec_load", 1), ("vec_load", 2),
-                  ("il", (0, 0, 0), 0, 4), ("il", (0, 1, 1), 0, 3)]
+                  ("il", (0, 0, 0), 0, 2), ("il", (0, 0, 1), 0, 2), ("il", (0, 1, 1), 0, 3)]
         pool_q += [("add1", ft) for ft in range(8) if ft != VECTOR_ADD_FT] + [("add2", ks[-1]) for ks in groups[:-1]]
 
         vec_q = [("memset",), ("vec_copy", 0)] + [("mult", e, b) for b in range(2) for e in range(E)]
         vec_q += [("mult", e, b) for pair in range(2) for b in (2, 3) for e in (2 * pair, 2 * pair + 1)]
-        vec_q += [("gate", 0), ("vec_copy", 1), ("il", (0, 1, 0), 0, 3), ("gate", 1), ("q_w", (0, 0, 0)), ("q_xe", 0, 0)]
+        vec_q += [("gate", 0), ("vec_copy", 1), ("q_w", (0, 0, 0)), ("gate", 1), ("q_xe", 0, 0)]
         between = [("q_w", (0, 1, 0)), ("q_xe", 0, 1), ("q_xe", 1, 0), ("q_xe", 1, 1), ("q_w", (0, 0, 1)), ("q_w", (0, 1, 1))]
         for step, name in zip(range(3, 9), between):
             vec_q += [name, ("gate", step)]
@@ -110,23 +110,27 @@ def tile_batchensemblerankoneexpertmixturemlp_x1_kernel(tc, x, wg, r1, w1, s1, r
             ("wide", 4, 1): [("add1", VECTOR_ADD_FT)],
             ("narrow", 1, 2): [("q_w", (1, 1, 0))],
             ("narrow", 3, 2): [("final", 0), ("final", 1)],
-            ("narrow", 5, 2): [("q_m", 1), ("q_w", (1, 1, 1)), ("final", 2), ("final", 3)],
+            ("narrow", 5, 2): [("q_m", 1), ("final", 2), ("final", 3), ("q_w", (1, 1, 1))],
             ("narrow", 6, 2): [("cp_p", 0, 0), ("q_m", 3), ("final", 4), ("final", 5)],
             ("narrow", 7, 2): [("q_m", 5)] + both("q_p", 0) + [("q_p", 1, 0), ("final", 6)],
             ("narrow", 7, 3): [("add2", 7), ("q_m", 6), ("q_p", 1, 1), ("final", 7)] + both("q_p", 2) + [("q_m", 7)],
         })
         vec_q += both("cp_p", LAST) + both("q_p", LAST)
 
-        act_q = [("warm",), ("il", (0, 0, 1), 0, 2), ("x_copy", 0), ("x_copy", 2), ("x_copy", 3), ("x_copy", 1), ("il", (0, 0, 1), 2, 4),
-                 ("il", (0, 1, 0), 3, 4), ("il", (0, 1, 1), 3, 4), ("il", (1, 0, 0), 0, 4), ("gate", 2), ("il", (1, 0, 1), 0, 4), ("il", (1, 1, 0), 0, 4)]
+        act_q = [("warm",), ("il", (0, 0, 0), 2, 4), ("il", (0, 0, 1), 2, 4), ("x_copy", 0), ("x_copy", 2), ("x_copy", 3), ("x_copy", 1),
+                 ("il", (0, 1, 0), 0, 4), ("il", (0, 1, 1), 3, 4), ("il", (1, 0, 0), 0, 2), ("gate", 2), ("il", (1, 0, 0), 2, 4),
+                 ("il", (1, 0, 1), 0, 4)]
         act_q += weave("gelu", {
-            ("wide", 5, 0): [("il", (1, 1, 1), 0, 1)],
-            ("narrow", 0, 2): [("il", (1, 1, 1), 1, 2)],
-            ("narrow", 1, 3): [("il", (1, 1, 1), 2, 3)],
-            ("narrow", 2, 3): [("il", (1, 1, 1), 3, 4)],
-            ("narrow", 7, 2): [("cp_p", 0, 1)] + both("cp_o", 0) + both("cp_p", 1),
-            ("narrow", 7, 3): both("cp_o", 1) + both("cp_p", 2) + both("cp_o", 2) + both("cp_e", LAST) + both("cp_o", LAST),
+            ("wide", 6, 0): [("il", (1, 1, 0), 0, 4)],
+            ("narrow", 2, 2): [("il", (1, 1, 1), 0, 1)],
+            ("narrow", 3, 3): [("il", (1, 1, 1), 1, 2)],
+            ("narrow", 4, 2): [("il", (1, 1, 1), 2, 3)],
+            ("narrow", 5, 2): [("il", (1, 1, 1), 3, 4)],
         })
+        act_q += [("cp_p", 0, 1)] + both("cp_o", 0)
+        for j in range(1, LAST):
+            act_q += both("cp_p", j) + both("cp_o", j)
+        act_q += both("cp_e", LAST) + both("cp_o", LAST)
         act_q += [("st_s", 2), ("st_s", 3)]
 
         pe_q = [("pe_warm",), ("vec_turn", 0)] + [("x_turn", b) for b in range(4)] + [("vec_turn", 1), ("logits",)]
@@ -271,7 +275,7 @@ def tile_batchensemblerankoneexpertmixturemlp_x1_kernel(tc, x, wg, r1, w1, s1, r
                 op(("q_xe", e, g), [("mult", e, 2 * g), ("mult", e, 2 * g + 1)], lambda e=e, g=g: quantize(
                     xe_codes[e][:, g, :], xe_scales[e][:, g, :], xe[2 * e + g][:]))
 
-        copies = [name for name in pool_q + act_q + vec_q if name[0] == "il"]
+        copies = [name for name in pool_q + act_q if name[0] == "il"]
         chunks = [name[1] for name in vec_q if name[0] == "q_w"]
 
         def interleave(chunk, q0, q1):
@@ -284,7 +288,7 @@ def tile_batchensemblerankoneexpertmixturemlp_x1_kernel(tc, x, wg, r1, w1, s1, r
                     in0=raw.rearrange("p t (c s) -> p s c t", s=4)[:, :, 32 * q0: 32 * q1],
                     scalar1=1.0, scalar2=0.0, op0=ALU.mult, op1=ALU.add)
             else:
-                (nc.vector.tensor_copy if ("il", chunk, q0, q1) in vec_q else nc.scalar.copy)(
+                nc.scalar.copy(
                     out=dst[:].rearrange("p (s a i) t -> p a s i t", s=4, i=2)[:, 16 * q0: 16 * q1],
                     in_=raw.rearrange("p t (a i s) -> p a s i t", s=4, i=2)[:, 16 * q0: 16 * q1])
 

from contextlib import ExitStack

import concourse.mybir as mybir
from concourse.masks import make_identity

T, D, F, O, E = 512, 1024, 1024, 1024, 4
FLOPS = 2 * E * T * D * F + 2 * T * F * O + 2 * T * D * E

F32 = mybir.dt.float32
BF16 = mybir.dt.bfloat16
I32 = mybir.dt.int32
U32 = mybir.dt.uint32
U8 = mybir.dt.uint8
FP8X4 = mybir.dt.float8_e4m3fn_x4
ALU = mybir.AluOpType
ACT = mybir.ActivationFunctionType
AX = mybir.AxisListType

P = 128
TILES = T // P
LAST = TILES - 1
STEPS = 2 * TILES
W_BUFS = 5
H_BUFS = 8
WARM_MATMULS = 4
VECTOR_ADD_FT = 3


def tile_batchensemblerankoneexpertmixturemlp_x1_kernel(tc, x, wg, r1, w1, s1, r2, w2, out_0, out_1, out_2):
    nc = tc.nc
    with ExitStack() as ctx:
        keep = ctx.enter_context(tc.tile_pool(name="keep", bufs=1))
        psum = ctx.enter_context(tc.psum_pool(name="psum", bufs=1))
        ctx.enter_context(tc.manual_schedule())

        def tiles(name, count, shape, dtype):
            return [keep.tile(shape, dtype, name="%s%d" % (name, i), align_bytes=64) for i in range(count)]

        def tile(name, shape, dtype):
            return keep.tile(shape, dtype, name=name, align_bytes=64)

        bank = [psum.tile([P, 512], F32, name="bank%d" % i) for i in range(8)]
        ident = tile("ident", [P, P], F32)
        zeros = tile("zeros", [P, 512], BF16)
        warm_in, warm_out = tiles("warm", 2, [P, 1], F32)
        vec_rows = tiles("vec_rows", 2, [P, 512], BF16)
        r1_col = tile("r1_col", [P, 8, 2, 2], BF16)
        sr_col = tile("sr_col", [P, 16, 4], F32)
        wg_sb = tile("wg_sb", [P, 2, 4, E], BF16)
        x_rows = tiles("x_rows", 4, [P, 2, 512], BF16)
        x_t = tile("x_t", [P, 2, T, 4], BF16)
        xe = tiles("xe", 2 * E, [P, T, 4], BF16)
        xe_codes = tiles("xe_codes", E, [P, 2, T], U32)
        xe_scales = tiles("xe_scales", E, [P, 2, T], U8)
        w_raw = tiles("w_raw", 4, [P, 4, 1024], BF16)
        w_grouped = tiles("w_grouped", W_BUFS, [P, 512, 4], BF16)
        w_codes = tiles("w_codes", 2, [P, 2, 1024], U32)
        w_scales = tiles("w_scales", 2, [P, 2, 1024], U8)
        gate_max, gate_sum, gate_inv = tiles("gate_stat", 3, [P, TILES], F32)
        gate_d, gate_th, gate_den, gate_rden, gate_ex, gate = tiles("gate_val", 6, [P, TILES, E], F32)
        h = tiles("h", H_BUFS, [P, 512], F32)
        acc = tile("acc", [P, 8, T], F32)
        term1 = tile("term1", [P, 4, T], F32)
        term2 = tiles("term2_", 2, [P, 8, P], F32)
        term3 = tiles("term3_", 2, [P, 4, P], F32)
        part = tile("part", [P, 8, P], F32)
        m_bf = tiles("m_bf", 2, [P, 2 * P, 4], BF16)
        m_codes = tile("m_codes", [P, TILES, 2, P], U32)
        m_scales = tile("m_scales", [P, TILES, 2, P], U8)
        out_sb = tiles("out_sb", 3, [P, O], F32)
        early_p = tiles("early_p", 2, [P, P, 4], F32)
        p_bf = tiles("p_bf", 4, [P, P, 4], BF16)
        p_codes = tile("p_codes", [P, 2, T], U32)
        p_scales = tile("p_scales", [P, 2, T], U8)

        wide = [("wide", ft, e) for ft in range(8) for e in range(2)]
        groups = [[2 * j, 2 * j + 1] for j in range(LAST)] + [[STEPS - 2], [STEPS - 1]]
        narrow = [("narrow", k, 2) for k in groups[0]]
        for i, ks in enumerate(groups):
            narrow += [("narrow", k, 3) for k in ks] + [("narrow", k, 2) for nxt in groups[i + 1: i + 2] for k in nxt]
        units = wide + narrow

        def weave(kind, extras):
            return [name for u in units for name in [(kind, u)] + extras.get(u, [])]

        def both(kind, j):
            return [(kind, j, 0), (kind, j, 1)]

        def group_of(k):
            return [ks for ks in groups if k in ks][0]

        sync_q = [("x_load", 0), ("vec_load", 0), ("w_load", 0, 0, 0, 1), ("x_load", 1), ("w_load", 0, 0, 1, 2), ("x_load", 2), ("x_load", 3),
                  ("w_load", 0, 1, 0, 2), ("w_load", 1, 0, 0, 2), ("w_load", 1, 1, 0, 2)]
        for j in range(LAST):
            sync_q += [("st_o", j, 0, 2), ("st_p", j)]
        sync_q += [("st_o", LAST, 0, 1), ("st_o", LAST, 1, 2), ("st_p", LAST), ("st_s", 0), ("st_s", 1)]

        pool_q = [("zeros",), ("ident",), ("wg_load",), ("vec_load", 1), ("vec_load", 2),
                  ("il", (0, 0, 0), 0, 2), ("il", (0, 0, 1), 0, 2), ("il", (0, 1, 1), 0, 3)]
        pool_q += [("add1", ft) for ft in range(8) if ft != VECTOR_ADD_FT] + [("add2", ks[-1]) for ks in groups[:-1]]

        vec_q = [("memset",), ("vec_copy", 0)] + [("mult", e, b) for b in range(2) for e in range(E)]
        vec_q += [("mult", e, b) for pair in range(2) for b in (2, 3) for e in (2 * pair, 2 * pair + 1)]
        vec_q += [("gate", 0), ("vec_copy", 1), ("q_w", (0, 0, 0)), ("gate", 1), ("q_xe", 0, 0)]
        between = [("q_w", (0, 1, 0)), ("q_xe", 0, 1), ("q_xe", 1, 0), ("q_xe", 1, 1), ("q_w", (0, 0, 1)), ("q_w", (0, 1, 1))]
        for step, name in zip(range(3, 9), between):
            vec_q += [name, ("gate", step)]
        vec_q += [("q_w", (1, 0, 0)), ("q_w", (1, 0, 1))] + both("q_xe", 2) + both("q_xe", 3)
        vec_q += weave("term", {
            ("wide", 4, 1): [("add1", VECTOR_ADD_FT)],
            ("narrow", 1, 2): [("q_w", (1, 1, 0))],
            ("narrow", 3, 2): [("final", 0), ("final", 1)],
            ("narrow", 5, 2): [("q_m", 1), ("final", 2), ("final", 3), ("q_w", (1, 1, 1))],
            ("narrow", 6, 2): [("cp_p", 0, 0), ("q_m", 3), ("final", 4), ("final", 5)],
            ("narrow", 7, 2): [("q_m", 5)] + both("q_p", 0) + [("q_p", 1, 0), ("final", 6)],
            ("narrow", 7, 3): [("add2", 7), ("q_m", 6), ("q_p", 1, 1), ("final", 7)] + both("q_p", 2) + [("q_m", 7)],
        })
        vec_q += both("cp_p", LAST) + both("q_p", LAST)

        act_q = [("warm",), ("il", (0, 0, 0), 2, 4), ("il", (0, 0, 1), 2, 4), ("x_copy", 0), ("x_copy", 2), ("x_copy", 3), ("x_copy", 1),
                 ("il", (0, 1, 0), 0, 4), ("il", (0, 1, 1), 3, 4), ("il", (1, 0, 0), 0, 2), ("gate", 2), ("il", (1, 0, 0), 2, 4),
                 ("il", (1, 0, 1), 0, 4)]
        act_q += weave("gelu", {
            ("wide", 6, 0): [("il", (1, 1, 0), 0, 4)],
            ("narrow", 2, 2): [("il", (1, 1, 1), 0, 1)],
            ("narrow", 3, 3): [("il", (1, 1, 1), 1, 2)],
            ("narrow", 4, 2): [("il", (1, 1, 1), 2, 3)],
            ("narrow", 5, 2): [("il", (1, 1, 1), 3, 4)],
        })
        act_q += [("cp_p", 0, 1)] + both("cp_o", 0)
        for j in range(1, LAST):
            act_q += both("cp_p", j) + both("cp_o", j)
        act_q += both("cp_e", LAST) + both("cp_o", LAST)
        act_q += [("st_s", 2), ("st_s", 3)]

        pe_q = [("pe_warm",), ("vec_turn", 0)] + [("x_turn", b) for b in range(4)] + [("vec_turn", 1), ("logits",)]
        pe_q += weave("mm", {
            ("wide", 1, 1): [("spread", 0), ("spread", 1)],
            ("narrow", 0, 2): [("spread", 2), ("spread", 3)],
            ("narrow", 7, 2): [("mm_p", 0, 0)],
            ("narrow", 7, 3): [("mm_p", 0, 1)] + both("mm_o", 0),
        })
        for j in range(1, LAST):
            pe_q += both("mm_p", j) + both("mm_o", j)
        pe_q += both("mm_e", LAST) + both("mm_open", LAST) + both("mm_o", LAST) + both("mm_p", LAST)

        bank_of = {("pe_warm",): 5, ("vec_turn", 0): 6, ("vec_turn", 1): 6, ("logits",): 7,
                   ("spread", 0): 4, ("spread", 1): 5, ("spread", 2): 2, ("spread", 3): 3}
        for b in range(4):
            bank_of["x_turn", b] = b
        for i, u in enumerate(wide):
            bank_of["mm", u] = [6, 7, 0, 1][i % 4]
        for i, u in enumerate(narrow):
            bank_of["mm", u] = [6, 7, 0][i % 3]
        for i, name in enumerate(name for j in range(LAST) for name in both("mm_p", j) + both("mm_o", j)):
            bank_of[name] = [1, 4, 5][i % 3]
        for og in range(2):
            bank_of["mm_open", LAST, og] = bank_of["mm_o", LAST, og] = [6, 7][og]
            bank_of["mm_e", LAST, og] = bank_of["mm_p", LAST, og] = [0, 2][og]

        def readers(name):
            kind = name[0]
            if kind == "x_turn":
                return [("x_copy", name[1])] + [("mult", e, name[1]) for e in range(E)]
            if kind == "vec_turn":
                return [("vec_copy", name[1])]
            if kind == "logits":
                return [("gate", 0), ("gate", 1)]
            if kind == "spread":
                return [("term", u) for u in units if u[2] == name[1]]
            if kind == "mm":
                return [("gelu", name[1])]
            if kind in ("pe_warm", "mm_open"):
                return []
            return [({"mm_p": "cp_p", "mm_o": "cp_o", "mm_e": "cp_e"}[kind],) + name[1:]]

        ops = {}

        def op(name, needs, fn):
            ops[name] = (needs, fn)

        def quantize(codes, scales, grouped):
            nc.vector.quantize_mx(out=codes.bitcast(FP8X4), scales=scales, in_=grouped.rearrange("p c t -> p (c t)"))

        def mx_pass(out, g, lhs, rhs, start, stop):
            nc.tensor.matmul_mx(
                out=out,
                lhsT=lhs[0][:, g, lhs[2]].bitcast(FP8X4), lhsT_scale=lhs[1][:, g, lhs[2]],
                rhs=rhs[0][:, g, rhs[2]].bitcast(FP8X4), rhs_scale=rhs[1][:, g, rhs[2]],
                start=start, stop=stop)

        def memsets():
            nc.vector.memset(vec_rows[0][:].bitcast(I32), 0)
            nc.vector.memset(vec_rows[1][:].bitcast(I32), 0)
            nc.vector.memset(warm_in[:], 0.0)

        def pe_warm():
            for i in range(WARM_MATMULS):
                nc.tensor.matmul(bank[5][:], lhsT=zeros[:, 0:P], rhs=zeros[:], start=True, stop=True)

        def vec_load(i):
            rows = (r1, s1, r2)[i].rearrange("e (g k) -> (e g) k", g=2)
            if i == 0:
                nc.sync.dma_start(out=vec_rows[0][0:8, :], in_=rows)
            else:
                nc.gpsimd.dma_start(out=vec_rows[1][8 * i - 8: 8 * i, :], in_=rows)

        def x_load(b):
            g, half = divmod(b, 2)
            rows = x[256 * half: 256 * half + 256, 512 * g: 512 * g + 512]
            nc.sync.dma_start(out=x_rows[b][:], in_=rows.rearrange("(j p) d -> p j d", p=P))

        def w_load(which, g, group0, group1):
            cols = slice(512 * group0, 512 * group1)
            rows = (w1, w2)[which][512 * g: 512 * g + 512, cols]
            nc.sync.dma_start(out=w_raw[2 * which + g][:, :, cols], in_=rows.rearrange("(p t) c -> p t c", t=4))

        op(("memset",), [], memsets)
        op(("zeros",), [], lambda: nc.gpsimd.memset(zeros[:].bitcast(I32), 0))
        op(("pe_warm",), [("zeros",)], pe_warm)
        op(("ident",), [], lambda: make_identity(nc, ident[:]))
        op(("warm",), [("memset",)], lambda: nc.scalar.activation(out=warm_out[:], in_=warm_in[:], func=ACT.Gelu))
        op(("wg_load",), [], lambda: nc.gpsimd.dma_start(
            out=wg_sb[:].rearrange("p g t e -> p g (t e)"), in_=wg.rearrange("(g p t) e -> p g (t e)", g=2, t=4)))
        for i in range(3):
            op(("vec_load", i), [("memset",)], lambda i=i: vec_load(i))
        for b in range(4):
            op(("x_load", b), [], lambda b=b: x_load(b))
        w_loads = [name for name in sync_q if name[0] == "w_load"]
        for name in w_loads:
            op(name, [], lambda name=name: w_load(*name[1:]))

        def x_turn(b):
            words = x_rows[b][:].bitcast(F32)
            for j in range(2):
                for u in range(2):
                    nc.tensor.transpose(bank[b][:, 256 * u + P * j: 256 * u + P * j + P], words[:, j, u:256:2], ident[:])

        def vec_turn(i):
            words = vec_rows[i][:].bitcast(F32)
            for u in range(2):
                nc.tensor.transpose(bank[6][:, P * u: P * u + P], words[:, u:256:2], ident[:])

        def vec_copy(i):
            cols = bank[6][:, 0:256].bitcast(BF16).rearrange("p (u r c) -> p r u c", u=2, c=2)
            if i == 0:
                nc.vector.tensor_copy(out=r1_col[:], in_=cols[:, 0:8])
            else:
                nc.vector.tensor_copy(out=sr_col[:].rearrange("p r (u c) -> p r u c", u=2), in_=cols[:, 0:16])

        def x_copy(b):
            g, half = divmod(b, 2)
            dst = x_t[:, g, 256 * half: 256 * half + 256, :].rearrange("p n t -> p (n t)").bitcast(F32)
            nc.scalar.copy(out=dst.rearrange("p (n u) -> p n u", u=2), in_=bank[b][:].rearrange("p (u n) -> p n u", u=2))

        def mult(e, b):
            g, half = divmod(b, 2)
            nc.vector.tensor_tensor(
                out=xe[2 * e + g][:, 256 * half: 256 * half + 256, :].rearrange("p n (u c) -> p n u c", u=2),
                in0=bank[b][:].bitcast(BF16).rearrange("p (u n c) -> p n u c", u=2, c=2),
                in1=r1_col[:, 2 * e + g].unsqueeze(1).to_broadcast([P, 256, 2, 2]),
                op=ALU.mult)

        for b in range(4):
            op(("x_turn", b), [("x_load", b), ("ident",)], lambda b=b: x_turn(b))
            op(("x_copy", b), [("x_turn", b)] + [("mult", e, b) for e in range(E) if b < 2], lambda b=b: x_copy(b))
            for e in range(E):
                op(("mult", e, b), [("x_turn", b), ("vec_copy", 0)] + ([("x_copy", b)] if b >= 2 else []), lambda e=e, b=b: mult(e, b))
        op(("vec_turn", 0), [("vec_load", 0), ("ident",)], lambda: vec_turn(0))
        op(("vec_turn", 1), [("vec_load", 1), ("vec_load", 2)], lambda: vec_turn(1))
        for i in range(2):
            op(("vec_copy", i), [("vec_turn", i)], lambda i=i: vec_copy(i))
        for e in range(E):
            for g in range(2):
                op(("q_xe", e, g), [("mult", e, 2 * g), ("mult", e, 2 * g + 1)], lambda e=e, g=g: quantize(
                    xe_codes[e][:, g, :], xe_scales[e][:, g, :], xe[2 * e + g][:]))

        copies = [name for name in pool_q + act_q if name[0] == "il"]
        chunks = [name[1] for name in vec_q if name[0] == "q_w"]

        def interleave(chunk, q0, q1):
            which, g, group = chunk
            raw = w_raw[2 * which + g][:, :, 512 * group: 512 * group + 512]
            dst = w_grouped[chunks.index(chunk) % W_BUFS]
            if ("il", chunk, q0, q1) in pool_q:
                nc.gpsimd.tensor_scalar(
                    out=dst[:].rearrange("p (s c) t -> p s c t", s=4)[:, :, 32 * q0: 32 * q1],
                    in0=raw.rearrange("p t (c s) -> p s c t", s=4)[:, :, 32 * q0: 32 * q1],
                    scalar1=1.0, scalar2=0.0, op0=ALU.mult, op1=ALU.add)
            else:
                nc.scalar.copy(
                    out=dst[:].rearrange("p (s a i) t -> p a s i t", s=4, i=2)[:, 16 * q0: 16 * q1],
                    in_=raw.rearrange("p t (a i s) -> p a s i t", s=4, i=2)[:, 16 * q0: 16 * q1])

        def q_w(chunk):
            which, g, group = chunk
            cols = slice(512 * group, 512 * group + 512)
            quantize(w_codes[which][:, g, cols], w_scales[which][:, g, cols], w_grouped[chunks.index(chunk) % W_BUFS][:])

        for name in copies:
            n = chunks.index(name[1])
            op(name, [load for load in w_loads if load[1:3] == name[1][:2] and load[3] <= name[1][2] < load[4]] + ([("q_w", chunks[n - W_BUFS])] if n >= W_BUFS else []),
               lambda name=name: interleave(*name[1:]))
        for chunk in chunks:
            op(("q_w", chunk), [name for name in copies if name[1] == chunk], lambda chunk=chunk: q_w(chunk))

        logits_ps = bank[7][:, 0: TILES * E].rearrange("p (j e) -> p j e", e=E)

        def logits():
            for j in range(TILES):
                for g in range(2):
                    for t in range(4):
                        nc.tensor.matmul(logits_ps[:, j, :], lhsT=x_t[:, g, P * j: P * j + P, t], rhs=wg_sb[:, g, t, :],
                                         start=(g == 0 and t == 0), stop=(g == 1 and t == 3))

        def over_experts(stat):
            return stat[:].unsqueeze(2).to_broadcast([P, TILES, E])

        def flat(val):
            return val[:].rearrange("p j e -> p (j e)")

        gate_steps = [
            lambda: nc.vector.tensor_reduce(out=gate_max[:], in_=logits_ps, axis=AX.X, op=ALU.max),
            lambda: nc.vector.tensor_tensor(out=gate_d[:], in0=logits_ps, in1=over_experts(gate_max), op=ALU.subtract),
            lambda: nc.scalar.activation(out=flat(gate_th), in_=flat(gate_d), func=ACT.Tanh, scale=0.5),
            lambda: nc.vector.tensor_scalar(out=flat(gate_den), in0=flat(gate_th), scalar1=-1.0, scalar2=1.0,
                                            op0=ALU.mult, op1=ALU.add),
            lambda: nc.vector.reciprocal(out=flat(gate_rden), in_=flat(gate_den)),
            lambda: nc.vector.scalar_tensor_tensor(out=flat(gate_ex), in0=flat(gate_th), scalar=1.0, in1=flat(gate_rden),
                                                   op0=ALU.add, op1=ALU.mult),
            lambda: nc.vector.tensor_reduce(out=gate_sum[:], in_=gate_ex[:], axis=AX.X, op=ALU.add),
            lambda: nc.vector.reciprocal(out=gate_inv[:], in_=gate_sum[:]),
            lambda: nc.vector.tensor_tensor(out=gate[:], in0=gate_ex[:], in1=over_experts(gate_inv), op=ALU.mult),
        ]

        def spread(e):
            for j in range(TILES):
                nc.tensor.transpose(bank[bank_of["spread", e]][:, P * j: P * j + P],
                                    gate[:, j, e: e + 1].to_broadcast([P, P]), ident[:])

        op(("logits",), [("x_copy", b) for b in range(4)] + [("wg_load",)], logits)
        for i, fn in enumerate(gate_steps):
            op(("gate", i), [("gate", i - 1) if i else ("logits",)], fn)
        for e in range(E):
            op(("spread", e), [("gate", len(gate_steps) - 1)], lambda e=e: spread(e))

        def unit_parts(u):
            if u[0] == "wide":
                return [(u[1], slice(0, T), slice(0, T))]
            j, g = divmod(u[1], 2)
            return [(4 * g + t, slice(P * j, P * j + P), slice(P * t, P * t + P)) for t in range(4)]

        def column(row0, e, ft):
            return sr_col[:, row0 + 2 * e + ft // 4, ft % 4: ft % 4 + 1]

        def mm(u):
            for ft, tokens, cols in unit_parts(u):
                for g in range(2):
                    mx_pass(bank[bank_of["mm", u]][:, cols], g, (w_codes[0], w_scales[0], slice(P * ft, P * ft + P)),
                            (xe_codes[u[2]], xe_scales[u[2]], tokens), g == 0, g == 1)

        def gelu(u):
            for ft, tokens, cols in unit_parts(u):
                nc.scalar.activation(out=h[units.index(u) % H_BUFS][:, cols], in_=bank[bank_of["mm", u]][:, cols],
                                     func=ACT.Gelu, scale=column(0, u[2], ft))

        def term(u):
            k, e = u[1], u[2]
            for ft, tokens, cols in unit_parts(u):
                dst = [acc[:, ft, :], term1[:, ft % 4, :], term2[k // 2 % 2][:, ft, :], term3[k % 2][:, ft % 4, :]][e]
                nc.vector.scalar_tensor_tensor(
                    out=dst, in0=h[units.index(u) % H_BUFS][:, cols], scalar=column(8, e, ft),
                    in1=bank[bank_of["spread", e]][:, tokens], op0=ALU.mult, op1=ALU.mult)

        for i, u in enumerate(units):
            k, e = u[1], u[2]
            group = k // 4 if u[0] == "wide" else k % 2
            op(("mm", u), [("q_xe", e, 0), ("q_xe", e, 1), ("q_w", (0, 0, group)), ("q_w", (0, 1, group))], lambda u=u: mm(u))
            op(("gelu", u), [("mm", u), ("vec_copy", 1)] + ([("term", units[i - H_BUFS])] if i >= H_BUFS else []), lambda u=u: gelu(u))
            needs = [("gelu", u), ("spread", e)]
            if e == 1 and k >= 4:
                needs.append(("add1", k - 4))
            if e == 2 and k >= 4:
                needs.append(("add2", group_of(k - 4)[-1]))
            if e == 3 and k >= 2:
                needs.append(("final", k - 2))
            op(("term", u), needs, lambda u=u: term(u))

        def adder(name):
            return nc.vector if name in vec_q else nc.gpsimd

        def part_row(k):
            return 4 * group_of(k).index(k)

        def add1(ft):
            adder(("add1", ft)).tensor_tensor(out=acc[:, ft, :], in0=acc[:, ft, :], in1=term1[:, ft % 4, :], op=ALU.add)

        def add2(ks):
            j, fts = ks[0] // 2, slice(4 * (ks[0] % 2), 4 * (ks[-1] % 2) + 4)
            adder(("add2", ks[-1])).tensor_tensor(out=part[:, 0: 4 * len(ks), :], in0=acc[:, fts, P * j: P * j + P],
                                                  in1=term2[j % 2][:, fts, :], op=ALU.add)

        def final(k):
            nc.vector.tensor_tensor(
                out=m_bf[k // 2 % 2][:, P * (k % 2): P * (k % 2) + P, :].rearrange("p (c i) t -> p c t i", i=4),
                in0=part[:, part_row(k): part_row(k) + 4, :].rearrange("p t (c i) -> p c t i", i=4),
                in1=term3[k % 2][:].rearrange("p t (c i) -> p c t i", i=4), op=ALU.add)

        def q_m(ks):
            j, g0, g1 = ks[0] // 2, ks[0] % 2, ks[-1] % 2 + 1
            quantize(m_codes[:, j, g0:g1, :].rearrange("p g n -> p (g n)"), m_scales[:, j, g0:g1, :].rearrange("p g n -> p (g n)"),
                     m_bf[j % 2][:, P * g0: P * g1, :])

        for ft in range(8):
            op(("add1", ft), [("term", ("wide", ft, e)) for e in range(2)], lambda ft=ft: add1(ft))
        for i, ks in enumerate(groups):
            op(("add2", ks[-1]), [("term", ("narrow", k, 2)) for k in ks] + [("add1", ft) for ft in range(8)]
               + [("final", k) for k in (groups[i - 1] if i else [])], lambda ks=ks: add2(ks))
            op(("q_m", ks[-1]), [("final", k) for k in ks], lambda ks=ks: q_m(ks))
            for k in ks:
                op(("final", k), [("term", ("narrow", k, 3)), ("add2", ks[-1])]
                   + ([("q_m", group_of(k - 4)[-1])] if k >= 4 else []), lambda k=k: final(k))

        def m_operand(j):
            return (m_codes[:, j], m_scales[:, j], slice(0, P))

        def mm_p(j, og, passes):
            for t in range(4):
                cols = slice(512 * og + P * t, 512 * og + P * t + P)
                for g in passes:
                    mx_pass(bank[bank_of["mm_p", j, og]][:, P * t: P * t + P], g, (w_codes[1], w_scales[1], cols), m_operand(j),
                            g == passes[0], g == passes[-1])

        def mm_o(j, og, passes):
            for g in passes:
                mx_pass(bank[bank_of["mm_o", j, og]][:], g, m_operand(j),
                        (w_codes[1], w_scales[1], slice(512 * og, 512 * og + 512)), g == 0, g == 1)

        def planes_view(j, og):
            return bank[bank_of["mm_p", j, og]][:].rearrange("p (t n) -> p n t", t=4)

        def p_tile(j, og):
            return p_bf[(2 * j + og) % 4]

        def cp_p(j, og):
            if j == LAST:
                nc.vector.tensor_tensor(out=p_tile(j, og)[:], in0=planes_view(j, og), in1=early_p[og][:], op=ALU.add)
            elif ("cp_p", j, og) in vec_q:
                nc.vector.tensor_copy(out=p_tile(j, og)[:], in_=planes_view(j, og))
            else:
                nc.scalar.copy(out=p_tile(j, og)[:], in_=planes_view(j, og))

        def cp_o(j, og):
            nc.scalar.copy(out=out_sb[j % 3][:, 512 * og: 512 * og + 512].rearrange("p (c s) -> p c s", s=4),
                           in_=bank[bank_of["mm_o", j, og]][:].rearrange("p (s c) -> p c s", s=4))

        def st_o(j, og0, og1):
            nc.sync.dma_start(out=out_0[P * j: P * j + P, 512 * og0: 512 * og1], in_=out_sb[j % 3][:, 512 * og0: 512 * og1])

        words_out = out_1.rearrange("g p m t -> p g (m t)").bitcast(I32)
        scales_out = out_2.rearrange("g q m -> q g m").bitcast(I32)

        def st_p(j):
            nc.sync.dma_start(out=words_out[:, :, P * j: P * j + P], in_=p_codes[:, :, P * j: P * j + P].bitcast(I32))

        def st_s(q):
            engine = nc.sync if ("st_s", q) in sync_q else nc.scalar
            engine.dma_start(out=scales_out[4 * q: 4 * q + 4], in_=p_scales[32 * q: 32 * q + 4].bitcast(I32))

        w2_ready = [("q_w", chunk) for chunk in chunks if chunk[0] == 1]
        for j in range(TILES):
            passes = [1] if j == LAST else [0, 1]
            for og in range(2):
                op(("mm_p", j, og), w2_ready + [("q_m", 2 * j + 1)], lambda j=j, og=og, passes=passes: mm_p(j, og, passes))
                op(("mm_o", j, og), w2_ready + [("q_m", 2 * j + 1)], lambda j=j, og=og, passes=passes: mm_o(j, og, passes))
                op(("cp_p", j, og), [("mm_p", j, og)] + ([("q_p", j - 2, og)] if j >= 2 else []), lambda j=j, og=og: cp_p(j, og))
                op(("cp_o", j, og), [("mm_o", j, og)] + ([("st_o", j - 3, 0, 2)] if j >= 3 else []), lambda j=j, og=og: cp_o(j, og))
                op(("q_p", j, og), [("cp_p", j, og)], lambda j=j, og=og: quantize(
                    p_codes[:, og, P * j: P * j + P], p_scales[:, og, P * j: P * j + P], p_tile(j, og)[:]))
            op(("st_p", j), both("q_p", j), lambda j=j: st_p(j))
        for og in range(2):
            op(("mm_e", LAST, og), [("q_m", 2 * LAST)], lambda og=og: mm_p(LAST, og, [0]))
            op(("mm_open", LAST, og), [("q_m", 2 * LAST)], lambda og=og: mm_o(LAST, og, [0]))
            op(("cp_e", LAST, og), [("mm_e", LAST, og)], lambda og=og: nc.scalar.copy(out=early_p[og][:], in_=planes_view(LAST, og)))
        for name in sync_q:
            if name[0] == "st_o":
                op(name, [("cp_o", name[1], og) for og in range(name[2], name[3])], lambda name=name: st_o(*name[1:]))
        for q in range(4):
            op(("st_s", q), [name for j in range(TILES) for name in both("q_p", j)], lambda q=q: st_s(q))

        bank_free = {}
        holder = {}
        for name in pe_q:
            bank_free[name] = readers(holder[bank_of[name]]) if bank_of[name] in holder else []
            holder[bank_of[name]] = name

        queues = [sync_q, pool_q, act_q, pe_q, vec_q]
        heads = [0] * len(queues)
        done = set()
        while any(heads[i] < len(q) for i, q in enumerate(queues)):
            written = len(done)
            for i, q in enumerate(queues):
                while heads[i] < len(q):
                    name = q[heads[i]]
                    needs, fn = ops[name]
                    if not all(n in done for n in needs + bank_free.get(name, [])):
                        break
                    fn()
                    done.add(name)
                    heads[i] = heads[i] + 1
            assert len(done) > written
